import numpy as np
import ml_dtypes


def mxq(x, axis, fmt="e4m3"):
    dtype, down = {"e4m3": (ml_dtypes.float8_e4m3fn, 7), "e5m2": (ml_dtypes.float8_e5m2, 14)}[fmt]
    v = np.moveaxis(np.asarray(x, np.float32).astype(ml_dtypes.bfloat16).astype(np.float64), axis, -1)
    blocks = v.reshape(v.shape[:-1] + (-1, 32))
    amax = np.abs(blocks).max(-1, keepdims=True)
    byte = np.maximum(np.where(amax > 0, np.frexp(amax)[1] - 1 + 127, 0) - down, 1)
    scale = np.exp2(byte - 127.0)
    codes = (blocks / scale).astype(np.float32).astype(dtype).astype(np.float64)
    return np.moveaxis((codes * scale).reshape(v.shape), -1, axis)


WIDE = False


def mx_kscale(k):
    if not WIDE:
        return np.ones(k)
    levels = np.array([10, -10, 5, -5, 0])
    if k % 512:
        return np.exp2(np.random.permutation(np.resize(levels, k // 32))).repeat(32)
    a = np.empty((k // 512, 16))
    for p in range(k // 512):
        a[p, :8] = np.random.permutation(np.resize(levels, 8))
        for g in range(8):
            far = levels[np.abs(levels - a[p, g]) >= 10]
            a[p, g + 8] = far[np.random.randint(len(far))]
    return np.exp2(a.ravel()).repeat(32)


def f64(x):
    return np.asarray(x).astype(np.float64)


def striped(idx):
    return np.tile(idx.reshape(-1, 16).T, (8, 1)).astype(np.uint16)


def unstriped(offs):
    return offs[:16].T.reshape(-1).astype(np.int64)


E2M1 = np.array([0.0, 0.5, 1.0, 1.5, 2.0, 3.0, 4.0, 6.0, -0.0, -0.5, -1.0, -1.5, -2.0, -3.0, -4.0, -6.0])


def pack_weight(w, fmt):
    k, n = w.shape
    w = f64(np.asarray(w, np.float32).astype(ml_dtypes.bfloat16)).reshape(k // 32, 32, n)
    amax = np.abs(w).max(1)
    if fmt == "e4m3":
        byte = np.frexp(amax)[1] - 1 + 127 - 7
    else:
        mant, ex = np.frexp(amax / 6.0)
        byte = np.where(mant > 0.5, ex, ex - 1) + 127
    byte = np.clip(np.where(amax > 0, byte, 1), 1, 254)
    scaled = (w * np.exp2(127.0 - byte)[:, None, :]).reshape(k, n).astype(np.float32)
    by_word = np.ascontiguousarray(scaled.reshape(k // 512, 128, 4, n).transpose(0, 1, 3, 2))
    if fmt == "e4m3":
        words = by_word.astype(ml_dtypes.float8_e4m3fn).view(np.uint8)
    else:
        c = by_word.astype(ml_dtypes.float4_e2m1fn).view(np.uint8) & 0xF
        words = (c[..., 0::2] | (c[..., 1::2] << 4)).reshape(k // 512, 128, 2 * n)
    return np.ascontiguousarray(words), np.ascontiguousarray(byte.astype(np.uint8).reshape(k // 512, 16, n))


def unpack_weight(words, scales, fmt):
    g, _, n = scales.shape
    words = np.ascontiguousarray(words).reshape(g, 128, n, -1)
    if fmt == "e4m3":
        vals = words.view(ml_dtypes.float8_e4m3fn).astype(np.float64)
    else:
        nib = np.empty((g, 128, n, 4), np.uint8)
        nib[..., 0::2] = words & 0xF
        nib[..., 1::2] = words >> 4
        vals = E2M1[nib]
    vals = vals * np.repeat(np.exp2(scales.astype(np.float64) - 127.0), 8, axis=1)[..., None]
    return vals.transpose(0, 1, 3, 2).reshape(g * 512, n)


def gelu(v):
    return 0.5 * v * (1.0 + np.tanh(np.sqrt(2.0 / np.pi) * (v + 0.044715 * v**3)))


def bf(x):
    return np.asarray(x, np.float32).astype(ml_dtypes.bfloat16)


def planes(Y):
    n, m = Y.shape
    b = f64(bf(Y)).reshape(n // 32, 32, m)
    amax = np.abs(b).max(1)
    byte = np.clip(np.where(amax > 0, np.frexp(amax)[1] - 1 + 127 - 7, 1), 1, 254)
    codes = (b * np.exp2(127.0 - byte)[:, None, :]).reshape(n, m).astype(np.float32).astype(ml_dtypes.float8_e4m3fn).view(np.uint8)
    words = codes.reshape(n // 512, 128, 4, m).transpose(0, 1, 3, 2)
    return np.ascontiguousarray(words), np.ascontiguousarray(byte.astype(np.uint8).reshape(n // 512, 16, m))


K, T, S, H, N = 1024, 4096, 1024, 1024, 256

def setup_inputs():
    n = np.random.standard_normal
    s = mx_kscale(K)[:, None]
    u = mx_kscale(H)[:, None]
    tab_words, tab_scales = pack_weight(n((K, T)) * s, "e4m3")
    offs = striped(np.random.permutation(T)[:S])
    w1_words, w1_scales = pack_weight(n((K, H)) / np.sqrt(K) / s, "e2m1")
    b1 = (0.3 * n(H)).astype(np.float32)
    gain = (np.random.uniform(0.6, 1.6, H) * u[:, 0]).astype(np.float32)
    w2 = (n((K, H)) / np.sqrt(K) / s * u.T).astype(np.float32)
    w3_words, w3_scales = pack_weight(0.4 * n((H, N)) / np.sqrt(H) / u, "e4m3")
    exposure = np.random.uniform(0.3, 2.0, (N, S)).astype(np.float32)
    return {"tab_words": tab_words, "tab_scales": tab_scales, "offs": offs,
            "w1_words": w1_words, "w1_scales": w1_scales, "b1": b1,
            "gain": gain, "w2": w2, "w3_words": w3_words,
            "w3_scales": w3_scales, "exposure": exposure}

def reference(tab_words, tab_scales, offs, w1_words, w1_scales, b1, gain, w2,
              w3_words, w3_scales, exposure):
    v = unpack_weight(tab_words, tab_scales, "e4m3")[:, unstriped(offs)]
    w1 = unpack_weight(w1_words, w1_scales, "e2m1")
    w3 = unpack_weight(w3_words, w3_scales, "e4m3")
    d = (w1.T @ v) + f64(b1)[:, None]
    act = 0.5 * d * (1.0 + np.tanh(0.7978845608 * (d + 0.044715 * d ** 3)))
    h = act * f64(gain)[:, None] + (mxq(f64(w2), 0, "e4m3").T @ v)
    words, scales = planes(h)
    y = f64(exposure) * np.exp(w3.T @ mxq(h, 0, "e4m3"))
    return y, h, words, scales

@@ -1,0 +1,245 @@
+from contextlib import ExitStack
+
+import concourse.mybir as mybir
+
+K, T, S, H, N = 1024, 4096, 1024, 1024, 256
+FLOPS = 2 * (2 * K * H * S + H * N * S)
+
+F32 = mybir.dt.float32
+BF16 = mybir.dt.bfloat16
+I32 = mybir.dt.int32
+U32 = mybir.dt.uint32
+U16 = mybir.dt.uint16
+U8 = mybir.dt.uint8
+FP8X4 = mybir.dt.float8_e4m3fn_x4
+FP4X4 = mybir.dt.float4_e2m1fn_x4
+ACT = mybir.ActivationFunctionType
+ALU = mybir.AluOpType
+
+P = 128
+PACK = 4
+PASS = P * PACK
+W = 512
+TAB0, W10, W30, ROW = 0, S, S + H, S + H + N
+
+
+def tile_list_telematics_claim_scoring_kernel(
+    tc, tab_words, tab_scales, offs, w1_words, w1_scales, b1, gain, w2, w3_words, w3_scales, exposure,
+    out_0, out_1, out_2, out_3,
+):
+    nc = tc.nc
+    with ExitStack() as ctx:
+        lists = ctx.enter_context(tc.tile_pool(name="lists", bufs=1))
+        keep = ctx.enter_context(tc.tile_pool(name="keep", bufs=1))
+        psum = ctx.enter_context(tc.psum_pool(name="psum", bufs=8))
+
+        def held(shape, dtype, name, tag=None):
+            return keep.tile(shape, dtype, name=name, tag=tag or name, align_bytes=64)
+
+        offsets = lists.tile([P, S // 16], U16, name="offsets")
+        nc.sync.dma_start(offsets[:], offs)
+
+        def scale_rows(scales):
+            return scales.rearrange("a q n -> q a n").bitcast(I32)
+
+        tab_rows = held([P, T], U8, "tab_rows", "slot_a")
+        w1_rows = held([P, H], U8, "w1_rows", "slot_c")
+        rows = held([P, ROW], U8, "rows")
+        planes = held([P, 2 * ROW], U8, "planes")
+        nc.sync.dma_start(tab_rows[0:32, :].bitcast(I32), scale_rows(tab_scales))
+        nc.sync.dma_start(w1_rows[0:32, :].bitcast(I32), scale_rows(w1_scales))
+        nc.sync.dma_start(rows[0:32, W30:ROW].bitcast(I32), scale_rows(w3_scales))
+        w1_raw = held([P, 2 * 2 * H], U8, "w1_raw", "slot_b")
+        nc.sync.dma_start(
+            w1_raw[:].bitcast(I32).rearrange("p (a c) -> p a c", a=2),
+            w1_words.rearrange("a p c -> p a c").bitcast(I32),
+        )
+        table = []
+        for a in range(2):
+            table.append(held([P, T], I32, "table%d" % a, "slot_t%d" % a))
+            nc.sync.dma_start(table[a][:], tab_words[a].rearrange("p t i -> p (t i)").bitcast(I32))
+
+        for lo, hi in ((32, 64), (64, P)):
+            nc.vector.memset(tab_rows[lo:hi, :].bitcast(I32), 0)
+            nc.vector.memset(w1_rows[lo:hi, :].bitcast(I32), 0)
+        nc.vector.memset(planes[:].bitcast(I32), 0)
+
+        picked_rows = held([P, S], U8, "picked_rows")
+        nc.vector.tensor_copy(picked_rows[:], tab_rows[:].indirect(offsets[:]))
+        nc.vector.tensor_copy(
+            rows[:, W10:W30].rearrange("p (g t m) -> p g t m", g=2, t=PACK),
+            w1_rows[:].rearrange("p (g m t) -> p g t m", g=2, t=PACK),
+        )
+        nc.vector.tensor_copy(rows[:, TAB0:W10].bitcast(I32), picked_rows[:].bitcast(I32))
+        for q in (0, 2, 1, 3):
+            nc.scalar.dma_start(
+                planes[32 * q : 32 * q + 4, :].bitcast(I32).rearrange("p (a c) -> p a c", a=2),
+                rows[8 * q : 8 * q + 8, :].bitcast(I32),
+            )
+        bias = held([P, 2, PACK], F32, "bias")
+        gains = held([P, 2, PACK], F32, "gains")
+        nc.scalar.dma_start(bias[:], b1.rearrange("(g p t) -> p g t", g=2, t=PACK))
+        nc.scalar.dma_start(gains[:], gain.rearrange("(g p t) -> p g t", g=2, t=PACK))
+
+        w1_codes = held([P, 2 * 2 * H], U8, "w1_codes")
+        nc.vector.tensor_copy(
+            w1_codes[:].bitcast(U16).rearrange("p (x t m) -> p x t m", x=4, t=PACK),
+            w1_raw[:].bitcast(U16).rearrange("p (x m t) -> p x t m", x=4, t=PACK),
+        )
+
+        picked = {}
+        for a in range(2):
+            for half in range(2):
+                picked[a, half] = held([P, W], U32, "picked%d%d" % (a, half))
+                nc.vector.tensor_copy(
+                    picked[a, half][:],
+                    table[a][:].bitcast(U32).indirect(offsets[:, half * W // 16 : (half + 1) * W // 16]),
+                )
+
+        w2_raw = {}
+        for g, a, tag in ((0, 0, "slot_a"), (0, 1, "slot_b"), (1, 0, "slot_c"), (1, 1, "slot_t0")):
+            w2_raw[g, a] = held([P, PACK, PASS], F32, "w2_raw%d%d" % (g, a), tag)
+            nc.sync.dma_start(
+                w2_raw[g, a][:],
+                w2[a * PASS : (a + 1) * PASS, g * PASS : (g + 1) * PASS].rearrange("(p j) c -> p j c", j=PACK),
+            )
+        expo = held([P, 2, S], F32, "expo", "slot_t1")
+        nc.sync.dma_start(expo[:], exposure.rearrange("(i p) j -> p i j", p=P))
+
+        w2_bf, w2_codes, w2_scales = {}, {}, {}
+
+        def round_w2(g, a, on_vector):
+            w2_bf[g, a] = held([P, PASS * PACK], BF16, "w2_bf%d%d" % (g, a))
+            dst = w2_bf[g, a][:].rearrange("p (t m j) -> p m j t", t=PACK, j=PACK)
+            src = w2_raw[g, a][:].rearrange("p j (m t) -> p m j t", t=PACK)
+            if on_vector:
+                nc.vector.tensor_copy(dst, src)
+            else:
+                nc.scalar.copy(dst, src)
+
+        def quantize_w2(g, a):
+            w2_codes[g, a] = held([P, PASS], U32, "w2_codes%d%d" % (g, a))
+            w2_scales[g, a] = held([P, PASS], U8, "w2_scales%d%d" % (g, a))
+            nc.vector.quantize_mx(out=w2_codes[g, a][:].bitcast(FP8X4), scales=w2_scales[g, a][:], in_=w2_bf[g, a][:])
+
+        def tab_plane(a, half):
+            return planes[:, a * ROW + TAB0 + half * W : a * ROW + TAB0 + (half + 1) * W]
+
+        act, h, h_bf, h_codes = {}, {}, {}, {}
+        h_scales = held([P, 2 * S], U8, "h_scales")
+
+        def gelu_branch(g, half):
+            for t in range(PACK):
+                col = g * PASS + t * P
+                acc = psum.tile([P, W], F32, name="acc")
+                for a in range(2):
+                    nc.tensor.matmul_mx(
+                        out=acc[:],
+                        lhsT=w1_codes[:, 2 * (a * H + col) : 2 * (a * H + col + P)].bitcast(FP4X4),
+                        lhsT_scale=planes[:, a * ROW + W10 + col : a * ROW + W10 + col + P],
+                        rhs=picked[a, half][:].bitcast(FP8X4),
+                        rhs_scale=tab_plane(a, half),
+                        start=(a == 0),
+                        stop=(a == 1),
+                    )
+                act[g, half, t] = held([P, W], F32, "act%d%d%d" % (g, half, t))
+                nc.scalar.activation(act[g, half, t][:], acc[:], ACT.Gelu_apprx_tanh, bias=bias[:, g, t : t + 1])
+
+        def linear_branch(g, half):
+            h[g, half] = held([P, PACK, W], F32, "h%d%d" % (g, half))
+            for t in range(PACK):
+                acc = psum.tile([P, W], F32, name="acc")
+                for a in range(2):
+                    nc.tensor.matmul_mx(
+                        out=acc[:],
+                        lhsT=w2_codes[g, a][:, t * P : (t + 1) * P].bitcast(FP8X4),
+                        lhsT_scale=w2_scales[g, a][:, t * P : (t + 1) * P],
+                        rhs=picked[a, half][:].bitcast(FP8X4),
+                        rhs_scale=tab_plane(a, half),
+                        start=(a == 0),
+                        stop=(a == 1),
+                    )
+                nc.vector.scalar_tensor_tensor(
+                    h[g, half][:, t, :], act[g, half, t][:], gains[:, g, t : t + 1], acc[:], ALU.mult, ALU.add
+                )
+            nc.sync.dma_start(
+                out_1[g * PASS : (g + 1) * PASS, half * W : (half + 1) * W].rearrange("(p t) j -> p t j", t=PACK),
+                h[g, half][:],
+            )
+
+        def round_h(g, half, on_vector):
+            h_bf[g, half] = held([P, W * PACK], BF16, "h_bf%d%d" % (g, half))
+            dst = h_bf[g, half][:].rearrange("p (c i t) -> p c t i", i=4, t=PACK)
+            src = h[g, half][:].rearrange("p t (c i) -> p c t i", i=4)
+            if on_vector:
+                nc.vector.tensor_copy(dst, src)
+            else:
+                nc.scalar.copy(dst, src)
+
+        def h_plane(g, half):
+            return h_scales[:, g * S + half * W : g * S + (half + 1) * W]
+
+        def quantize_h(g, half):
+            h_codes[g, half] = held([P, W], U32, "h_codes%d%d" % (g, half))
+            nc.vector.quantize_mx(out=h_codes[g, half][:].bitcast(FP8X4), scales=h_plane(g, half), in_=h_bf[g, half][:])
+            nc.sync.dma_start(
+                out_2[g].rearrange("p m t -> p (m t)").bitcast(I32)[:, half * W : (half + 1) * W],
+                h_codes[g, half][:].bitcast(I32),
+            )
+
+        def head(half):
+            cols = slice(half * W, (half + 1) * W)
+            for i in range(N // P):
+                acc = psum.tile([P, W], F32, name="acc")
+                for g in range(2):
+                    nc.tensor.matmul_mx(
+                        out=acc[:],
+                        lhsT=w3_codes[:, g * N + i * P : g * N + (i + 1) * P].bitcast(FP8X4),
+                        lhsT_scale=planes[:, g * ROW + W30 + i * P : g * ROW + W30 + (i + 1) * P],
+                        rhs=h_codes[g, half][:].bitcast(FP8X4),
+                        rhs_scale=h_plane(g, half),
+                        start=(g == 0),
+                        stop=(g == 1),
+                    )
+                rate = held([P, W], F32, "rate%d%d" % (half, i))
+                nc.scalar.activation(rate[:], acc[:], ACT.Exp)
+                claims = held([P, W], F32, "claims%d%d" % (half, i))
+                nc.vector.tensor_tensor(claims[:], rate[:], expo[:, i, cols], ALU.mult)
+                nc.sync.dma_start(out_0[i * P : (i + 1) * P, cols], claims[:])
+
+        gelu_branch(0, 0)
+        gelu_branch(0, 1)
+        round_w2(0, 0, True)
+        quantize_w2(0, 0)
+        round_w2(0, 1, True)
+        quantize_w2(0, 1)
+        w3_codes = held([P, 2 * N], I32, "w3_codes", "slot_a")
+        nc.sync.dma_start(
+            w3_codes[:].rearrange("p (a c) -> p a c", a=2),
+            w3_words.rearrange("a p c i -> p a (c i)").bitcast(I32),
+        )
+        linear_branch(0, 0)
+        gelu_branch(1, 0)
+        round_w2(1, 0, True)
+        linear_branch(0, 1)
+        gelu_branch(1, 1)
+        quantize_w2(1, 0)
+        round_w2(1, 1, False)
+        quantize_w2(1, 1)
+        round_h(0, 0, True)
+        round_h(0, 1, False)
+        linear_branch(1, 0)
+        quantize_h(0, 0)
+        round_h(1, 0, False)
+        quantize_h(0, 1)
+        linear_branch(1, 1)
+        quantize_h(1, 0)
+        round_h(1, 1, True)
+        head(0)
+        quantize_h(1, 1)
+        for q in (0, 2, 1, 3):
+            nc.sync.dma_start(
+                out_3[:, 4 * q : 4 * q + 4, :].rearrange("g r j -> r g j").bitcast(I32),
+                h_scales[32 * q : 32 * q + 4, :].bitcast(I32).rearrange("p (g j) -> p g j", g=2),
+            )
+        head(1)

@@ -20,6 +20,7 @@ P = 128
 PACK = 4
 PASS = P * PACK
 W = 512
+R0 = 96
 TAB0, W10, W30, ROW = 0, S, S + H, S + H + N
 
 
@@ -42,13 +43,13 @@ def tile_list_telematics_claim_scoring_kernel(
         def scale_rows(scales):
             return scales.rearrange("a q n -> q a n").bitcast(I32)
 
-        tab_rows = held([P, T], U8, "tab_rows", "slot_a")
-        w1_rows = held([P, H], U8, "w1_rows", "slot_c")
-        rows = held([P, ROW], U8, "rows")
+        tab_rows = held([P, T], U8, "tab_rows")
+        w1_rows = held([P, H], U8, "w1_rows")
+        rows = held([P, ROW], U8, "rows", "slot_r")
         planes = held([P, 2 * ROW], U8, "planes")
-        nc.sync.dma_start(tab_rows[0:32, :].bitcast(I32), scale_rows(tab_scales))
-        nc.sync.dma_start(w1_rows[0:32, :].bitcast(I32), scale_rows(w1_scales))
-        nc.sync.dma_start(rows[0:32, W30:ROW].bitcast(I32), scale_rows(w3_scales))
+        nc.sync.dma_start(tab_rows[R0:P, :].bitcast(I32), scale_rows(tab_scales))
+        nc.sync.dma_start(w1_rows[R0:P, :].bitcast(I32), scale_rows(w1_scales))
+        nc.sync.dma_start(rows[R0:P, W30:ROW].bitcast(I32), scale_rows(w3_scales))
         w1_raw = held([P, 2 * 2 * H], U8, "w1_raw", "slot_b")
         nc.sync.dma_start(
             w1_raw[:].bitcast(I32).rearrange("p (a c) -> p a c", a=2),
@@ -59,9 +60,8 @@ def tile_list_telematics_claim_scoring_kernel(
             table.append(held([P, T], I32, "table%d" % a, "slot_t%d" % a))
             nc.sync.dma_start(table[a][:], tab_words[a].rearrange("p t i -> p (t i)").bitcast(I32))
 
-        for lo, hi in ((32, 64), (64, P)):
-            nc.vector.memset(tab_rows[lo:hi, :].bitcast(I32), 0)
-            nc.vector.memset(w1_rows[lo:hi, :].bitcast(I32), 0)
+        nc.vector.memset(tab_rows[0:R0, :].bitcast(I32), 0)
+        nc.vector.memset(w1_rows[0:R0, :].bitcast(I32), 0)
         nc.vector.memset(planes[:].bitcast(I32), 0)
 
         picked_rows = held([P, S], U8, "picked_rows")
@@ -74,7 +74,7 @@ def tile_list_telematics_claim_scoring_kernel(
         for q in (0, 2, 1, 3):
             nc.scalar.dma_start(
                 planes[32 * q : 32 * q + 4, :].bitcast(I32).rearrange("p (a c) -> p a c", a=2),
-                rows[8 * q : 8 * q + 8, :].bitcast(I32),
+                rows[R0 + 8 * q : R0 + 8 * q + 8, :].bitcast(I32),
             )
         bias = held([P, 2, PACK], F32, "bias")
         gains = held([P, 2, PACK], F32, "gains")
@@ -97,25 +97,29 @@ def tile_list_telematics_claim_scoring_kernel(
                 )
 
         w2_raw = {}
-        for g, a, tag in ((0, 0, "slot_a"), (0, 1, "slot_b"), (1, 0, "slot_c"), (1, 1, "slot_t0")):
+        for g, a, tag in ((0, 0, "slot_b"), (0, 1, "slot_t0"), (1, 0, "slot_r"), (1, 1, "slot_t1")):
             w2_raw[g, a] = held([P, PACK, PASS], F32, "w2_raw%d%d" % (g, a), tag)
             nc.sync.dma_start(
                 w2_raw[g, a][:],
                 w2[a * PASS : (a + 1) * PASS, g * PASS : (g + 1) * PASS].rearrange("(p j) c -> p j c", j=PACK),
             )
-        expo = held([P, 2, S], F32, "expo", "slot_t1")
-        nc.sync.dma_start(expo[:], exposure.rearrange("(i p) j -> p i j", p=P))
 
         w2_bf, w2_codes, w2_scales = {}, {}, {}
 
-        def round_w2(g, a, on_vector):
-            w2_bf[g, a] = held([P, PASS * PACK], BF16, "w2_bf%d%d" % (g, a))
+        def rounded(engine, dst, src):
+            if engine == "vector":
+                nc.vector.tensor_copy(dst, src)
+            elif engine == "scalar":
+                nc.scalar.copy(dst, src)
+            else:
+                nc.gpsimd.tensor_scalar(dst, src, 1.0, 0.0, ALU.mult, ALU.add)
+
+        def round_w2(g, a, engine, tag=None, lo=0, hi=P):
+            if lo == 0:
+                w2_bf[g, a] = held([P, PASS * PACK], BF16, "w2_bf%d%d" % (g, a), tag)
             dst = w2_bf[g, a][:].rearrange("p (t m j) -> p m j t", t=PACK, j=PACK)
             src = w2_raw[g, a][:].rearrange("p j (m t) -> p m j t", t=PACK)
-            if on_vector:
-                nc.vector.tensor_copy(dst, src)
-            else:
-                nc.scalar.copy(dst, src)
+            rounded(engine, dst[:, lo:hi], src[:, lo:hi])
 
         def quantize_w2(g, a):
             w2_codes[g, a] = held([P, PASS], U32, "w2_codes%d%d" % (g, a))
@@ -128,53 +132,76 @@ def tile_list_telematics_claim_scoring_kernel(
         act, h, h_bf, h_codes = {}, {}, {}, {}
         h_scales = held([P, 2 * S], U8, "h_scales")
 
-        def gelu_branch(g, half):
-            for t in range(PACK):
-                col = g * PASS + t * P
-                acc = psum.tile([P, W], F32, name="acc")
-                for a in range(2):
-                    nc.tensor.matmul_mx(
-                        out=acc[:],
-                        lhsT=w1_codes[:, 2 * (a * H + col) : 2 * (a * H + col + P)].bitcast(FP4X4),
-                        lhsT_scale=planes[:, a * ROW + W10 + col : a * ROW + W10 + col + P],
-                        rhs=picked[a, half][:].bitcast(FP8X4),
-                        rhs_scale=tab_plane(a, half),
-                        start=(a == 0),
-                        stop=(a == 1),
-                    )
-                act[g, half, t] = held([P, W], F32, "act%d%d%d" % (g, half, t))
-                nc.scalar.activation(act[g, half, t][:], acc[:], ACT.Gelu_apprx_tanh, bias=bias[:, g, t : t + 1])
+        pre = {}
 
-        def linear_branch(g, half):
-            h[g, half] = held([P, PACK, W], F32, "h%d%d" % (g, half))
-            for t in range(PACK):
-                acc = psum.tile([P, W], F32, name="acc")
-                for a in range(2):
-                    nc.tensor.matmul_mx(
-                        out=acc[:],
-                        lhsT=w2_codes[g, a][:, t * P : (t + 1) * P].bitcast(FP8X4),
-                        lhsT_scale=w2_scales[g, a][:, t * P : (t + 1) * P],
-                        rhs=picked[a, half][:].bitcast(FP8X4),
-                        rhs_scale=tab_plane(a, half),
-                        start=(a == 0),
-                        stop=(a == 1),
-                    )
-                nc.vector.scalar_tensor_tensor(
-                    h[g, half][:, t, :], act[g, half, t][:], gains[:, g, t : t + 1], acc[:], ALU.mult, ALU.add
-                )
-            nc.sync.dma_start(
-                out_1[g * PASS : (g + 1) * PASS, half * W : (half + 1) * W].rearrange("(p t) j -> p t j", t=PACK),
-                h[g, half][:],
+        def w1_pass(g, half, t, a):
+            col = g * PASS + t * P
+            if a == 0:
+                pre[g, half, t] = psum.tile([P, W], F32, name="acc")
+            nc.tensor.matmul_mx(
+                out=pre[g, half, t][:],
+                lhsT=w1_codes[:, 2 * (a * H + col) : 2 * (a * H + col + P)].bitcast(FP4X4),
+                lhsT_scale=planes[:, a * ROW + W10 + col : a * ROW + W10 + col + P],
+                rhs=picked[a, half][:].bitcast(FP8X4),
+                rhs_scale=tab_plane(a, half),
+                start=(a == 0),
+                stop=(a == 1),
             )
 
-        def round_h(g, half, on_vector):
-            h_bf[g, half] = held([P, W * PACK], BF16, "h_bf%d%d" % (g, half))
+        def gelu(g, half, t):
+            act[g, half, t] = held([P, W], F32, "act%d%d%d" % (g, half, t))
+            nc.scalar.activation(act[g, half, t][:], pre[g, half, t][:], ACT.Gelu_apprx_tanh, bias=bias[:, g, t : t + 1])
+
+        def gelu_branch(g, half):
+            for t in range(PACK):
+                w1_pass(g, half, t, 0)
+                w1_pass(g, half, t, 1)
+                gelu(g, half, t)
+
+        h_whole = held([P, PACK, S], F32, "h_whole")
+        for half in range(2):
+            h[0, half] = h_whole[:, :, half * W : (half + 1) * W]
+            h[1, half] = held([P, PACK, W], F32, "h1%d" % half)[:]
+
+        def feature_tile(g, half, t):
+            acc = psum.tile([P, W], F32, name="acc")
+            for a in range(2):
+                nc.tensor.matmul_mx(
+                    out=acc[:],
+                    lhsT=w2_codes[g, a][:, t * P : (t + 1) * P].bitcast(FP8X4),
+                    lhsT_scale=w2_scales[g, a][:, t * P : (t + 1) * P],
+                    rhs=picked[a, half][:].bitcast(FP8X4),
+                    rhs_scale=tab_plane(a, half),
+                    start=(a == 0),
+                    stop=(a == 1),
+                )
+            nc.vector.scalar_tensor_tensor(
+                h[g, half][:, t, :], act[g, half, t][:], gains[:, g, t : t + 1], acc[:], ALU.mult, ALU.add
+            )
+
+        def feature_rows(g):
+            return out_1[g * PASS : (g + 1) * PASS, :].rearrange("(p t) j -> p t j", t=PACK)
+
+        def first_group_pair(u):
+            for t in (2 * u, 2 * u + 1):
+                for half in range(2):
+                    feature_tile(0, half, t)
+            nc.sync.dma_start(feature_rows(0)[:, 2 * u : 2 * u + 2, :], h_whole[:, 2 * u : 2 * u + 2, :])
+
+        def linear_branch(g, half):
+            for t in range(PACK):
+                feature_tile(g, half, t)
+            nc.sync.dma_start(feature_rows(g)[:, :, half * W : (half + 1) * W], h[g, half])
+
+        def round_h(g, half, engine, lo=0, hi=P):
+            if lo == 0:
+                h_bf[g, half] = held([P, W * PACK], BF16, "h_bf%d%d" % (g, half))
             dst = h_bf[g, half][:].rearrange("p (c i t) -> p c t i", i=4, t=PACK)
-            src = h[g, half][:].rearrange("p t (c i) -> p c t i", i=4)
-            if on_vector:
-                nc.vector.tensor_copy(dst, src)
-            else:
-                nc.scalar.copy(dst, src)
+            src = h[g, half].rearrange("p t (c i) -> p c t i", i=4)
+            rounded(engine, dst[:, lo:hi], src[:, lo:hi])
+
+        def store_h(g, half):
+            nc.sync.dma_start(feature_rows(g)[:, :, half * W : (half + 1) * W], h[g, half])
 
         def h_plane(g, half):
             return h_scales[:, g * S + half * W : g * S + (half + 1) * W]
@@ -207,39 +234,52 @@ def tile_list_telematics_claim_scoring_kernel(
                 nc.vector.tensor_tensor(claims[:], rate[:], expo[:, i, cols], ALU.mult)
                 nc.sync.dma_start(out_0[i * P : (i + 1) * P, cols], claims[:])
 
-        gelu_branch(0, 0)
-        gelu_branch(0, 1)
-        round_w2(0, 0, True)
-        quantize_w2(0, 0)
-        round_w2(0, 1, True)
-        quantize_w2(0, 1)
-        w3_codes = held([P, 2 * N], I32, "w3_codes", "slot_a")
-        nc.sync.dma_start(
-            w3_codes[:].rearrange("p (a c) -> p a c", a=2),
-            w3_words.rearrange("a p c i -> p a (c i)").bitcast(I32),
-        )
-        linear_branch(0, 0)
-        gelu_branch(1, 0)
-        round_w2(1, 0, True)
-        linear_branch(0, 1)
-        gelu_branch(1, 1)
-        quantize_w2(1, 0)
-        round_w2(1, 1, False)
-        quantize_w2(1, 1)
-        round_h(0, 0, True)
-        round_h(0, 1, False)
-        linear_branch(1, 0)
-        quantize_h(0, 0)
-        round_h(1, 0, False)
-        quantize_h(0, 1)
-        linear_branch(1, 1)
-        quantize_h(1, 0)
-        round_h(1, 1, True)
-        head(0)
-        quantize_h(1, 1)
-        for q in (0, 2, 1, 3):
+        def load_w3():
             nc.sync.dma_start(
-                out_3[:, 4 * q : 4 * q + 4, :].rearrange("g r j -> r g j").bitcast(I32),
-                h_scales[32 * q : 32 * q + 4, :].bitcast(I32).rearrange("p (g j) -> p g j", g=2),
+                w3_codes[:].rearrange("p (a c) -> p a c", a=2),
+                w3_words.rearrange("a p c i -> p a (c i)").bitcast(I32),
             )
+
+        def store_scales():
+            for q in (0, 2, 1, 3):
+                nc.sync.dma_start(
+                    out_3[:, 4 * q : 4 * q + 4, :].rearrange("g r j -> r g j").bitcast(I32),
+                    h_scales[32 * q : 32 * q + 4, :].bitcast(I32).rearrange("p (g j) -> p g j", g=2),
+                )
+
+        for half in range(2):
+            for t in range(PACK):
+                w1_pass(0, half, t, 0)
+        for half in range(2):
+            for t in range(PACK):
+                w1_pass(0, half, t, 1)
+                gelu(0, half, t)
+        round_w2(0, 0, "vector")
+        quantize_w2(0, 0)
+        round_w2(0, 1, "vector", "slot_q")
+        quantize_w2(0, 1)
+        w3_codes = held([P, 2 * N], I32, "w3_codes", "slot_b")
+        load_w3()
+        expo = held([P, 2, S], F32, "expo", "slot_t0")
+        nc.sync.dma_start(expo[:], exposure.rearrange("(i p) j -> p i j", p=P))
+        gelu_branch(1, 0)
+        gelu_branch(1, 1)
+        round_w2(1, 0, "vector")
+        first_group_pair(0)
+        quantize_w2(1, 0)
+        round_w2(1, 1, "scalar")
+        quantize_w2(1, 1)
+        first_group_pair(1)
+        round_h(0, 0, "scalar")
+        linear_branch(1, 0)
+        round_h(0, 1, "scalar")
+        quantize_h(0, 0)
+        round_h(1, 0, "scalar")
+        linear_branch(1, 1)
+        quantize_h(0, 1)
+        quantize_h(1, 0)
+        round_h(1, 1, "vector")
+        quantize_h(1, 1)
+        head(0)
+        store_scales()
         head(1)

@@ -44,27 +44,36 @@ def tile_list_telematics_claim_scoring_kernel(
             return scales.rearrange("a q n -> q a n").bitcast(I32)
 
         tab_rows = held([P, T], U8, "tab_rows")
-        w1_rows = held([P, H], U8, "w1_rows")
-        rows = held([P, ROW], U8, "rows", "slot_r")
+        w1_rows = held([P, H], U8, "w1_rows", "slot_c")
+        rows = held([P, ROW], U8, "rows")
         planes = held([P, 2 * ROW], U8, "planes")
         nc.sync.dma_start(tab_rows[R0:P, :].bitcast(I32), scale_rows(tab_scales))
         nc.sync.dma_start(w1_rows[R0:P, :].bitcast(I32), scale_rows(w1_scales))
         nc.sync.dma_start(rows[R0:P, W30:ROW].bitcast(I32), scale_rows(w3_scales))
-        w1_raw = held([P, 2 * 2 * H], U8, "w1_raw", "slot_b")
-        nc.sync.dma_start(
-            w1_raw[:].bitcast(I32).rearrange("p (a c) -> p a c", a=2),
-            w1_words.rearrange("a p c -> p a c").bitcast(I32),
-        )
-        table = []
+        w1_raw = []
         for a in range(2):
+            w1_raw.append(held([P, 2 * H], U8, "w1_raw%d" % a, "slot_w%d" % a))
+            nc.sync.dma_start(w1_raw[a][:].bitcast(I32), w1_words[a].bitcast(I32))
+        table = []
+
+        def load_table(a):
             table.append(held([P, T], I32, "table%d" % a, "slot_t%d" % a))
             nc.sync.dma_start(table[a][:], tab_words[a].rearrange("p t i -> p (t i)").bitcast(I32))
+
+        load_table(0)
+        gains = held([P, 2, PACK], F32, "gains")
+        nc.sync.dma_start(gains[:], gain.rearrange("(g p t) -> p g t", g=2, t=PACK))
+        w3_codes = held([P, 2 * N], I32, "w3_codes")
+        nc.sync.dma_start(
+            w3_codes[:].rearrange("p (a c) -> p a c", a=2),
+            w3_words.rearrange("a p c i -> p a (c i)").bitcast(I32),
+        )
 
         nc.vector.memset(tab_rows[0:R0, :].bitcast(I32), 0)
         nc.vector.memset(w1_rows[0:R0, :].bitcast(I32), 0)
         nc.vector.memset(planes[:].bitcast(I32), 0)
 
-        picked_rows = held([P, S], U8, "picked_rows")
+        picked_rows = held([P, S], U8, "picked_rows", "slot_t1")
         nc.vector.tensor_copy(picked_rows[:], tab_rows[:].indirect(offsets[:]))
         nc.vector.tensor_copy(
             rows[:, W10:W30].rearrange("p (g t m) -> p g t m", g=2, t=PACK),
@@ -72,20 +81,20 @@ def tile_list_telematics_claim_scoring_kernel(
         )
         nc.vector.tensor_copy(rows[:, TAB0:W10].bitcast(I32), picked_rows[:].bitcast(I32))
         for q in (0, 2, 1, 3):
-            nc.scalar.dma_start(
+            nc.sync.dma_start(
                 planes[32 * q : 32 * q + 4, :].bitcast(I32).rearrange("p (a c) -> p a c", a=2),
                 rows[R0 + 8 * q : R0 + 8 * q + 8, :].bitcast(I32),
             )
+        load_table(1)
         bias = held([P, 2, PACK], F32, "bias")
-        gains = held([P, 2, PACK], F32, "gains")
         nc.scalar.dma_start(bias[:], b1.rearrange("(g p t) -> p g t", g=2, t=PACK))
-        nc.scalar.dma_start(gains[:], gain.rearrange("(g p t) -> p g t", g=2, t=PACK))
 
-        w1_codes = held([P, 2 * 2 * H], U8, "w1_codes")
-        nc.vector.tensor_copy(
-            w1_codes[:].bitcast(U16).rearrange("p (x t m) -> p x t m", x=4, t=PACK),
-            w1_raw[:].bitcast(U16).rearrange("p (x m t) -> p x t m", x=4, t=PACK),
-        )
+        w1_codes = held([P, 2 * 2 * H], U8, "w1_codes", "slot_c")
+        for a in range(2):
+            nc.vector.tensor_copy(
+                w1_codes[:, a * 2 * H : (a + 1) * 2 * H].bitcast(U16).rearrange("p (g t m) -> p g t m", g=2, t=PACK),
+                w1_raw[a][:].bitcast(U16).rearrange("p (g m t) -> p g t m", g=2, t=PACK),
+            )
 
         picked = {}
         for a in range(2):
@@ -97,7 +106,7 @@ def tile_list_telematics_claim_scoring_kernel(
                 )
 
         w2_raw = {}
-        for g, a, tag in ((0, 0, "slot_b"), (0, 1, "slot_t0"), (1, 0, "slot_r"), (1, 1, "slot_t1")):
+        for g, a, tag in ((0, 0, "slot_w0"), (0, 1, "slot_w1"), (1, 0, "slot_t0"), (1, 1, "slot_t1")):
             w2_raw[g, a] = held([P, PACK, PASS], F32, "w2_raw%d%d" % (g, a), tag)
             nc.sync.dma_start(
                 w2_raw[g, a][:],
@@ -117,12 +126,12 @@ def tile_list_telematics_claim_scoring_kernel(
         def round_w2(g, a, engine, tag=None, lo=0, hi=P):
             if lo == 0:
                 w2_bf[g, a] = held([P, PASS * PACK], BF16, "w2_bf%d%d" % (g, a), tag)
-            dst = w2_bf[g, a][:].rearrange("p (t m j) -> p m j t", t=PACK, j=PACK)
-            src = w2_raw[g, a][:].rearrange("p j (m t) -> p m j t", t=PACK)
+            dst = w2_bf[g, a][:].rearrange("p (t m j) -> p m t j", t=PACK, j=PACK)
+            src = w2_raw[g, a][:].rearrange("p j (m t) -> p m t j", t=PACK)
             rounded(engine, dst[:, lo:hi], src[:, lo:hi])
 
-        def quantize_w2(g, a):
-            w2_codes[g, a] = held([P, PASS], U32, "w2_codes%d%d" % (g, a))
+        def quantize_w2(g, a, tag=None):
+            w2_codes[g, a] = held([P, PASS], U32, "w2_codes%d%d" % (g, a), tag)
             w2_scales[g, a] = held([P, PASS], U8, "w2_scales%d%d" % (g, a))
             nc.vector.quantize_mx(out=w2_codes[g, a][:].bitcast(FP8X4), scales=w2_scales[g, a][:], in_=w2_bf[g, a][:])
 
@@ -158,9 +167,8 @@ def tile_list_telematics_claim_scoring_kernel(
                 w1_pass(g, half, t, 1)
                 gelu(g, half, t)
 
-        h_whole = held([P, PACK, S], F32, "h_whole")
         for half in range(2):
-            h[0, half] = h_whole[:, :, half * W : (half + 1) * W]
+            h[0, half] = held([P, PACK, W], F32, "h0%d" % half)[:]
             h[1, half] = held([P, PACK, W], F32, "h1%d" % half)[:]
 
         def feature_tile(g, half, t):
@@ -182,12 +190,6 @@ def tile_list_telematics_claim_scoring_kernel(
         def feature_rows(g):
             return out_1[g * PASS : (g + 1) * PASS, :].rearrange("(p t) j -> p t j", t=PACK)
 
-        def first_group_pair(u):
-            for t in (2 * u, 2 * u + 1):
-                for half in range(2):
-                    feature_tile(0, half, t)
-            nc.sync.dma_start(feature_rows(0)[:, 2 * u : 2 * u + 2, :], h_whole[:, 2 * u : 2 * u + 2, :])
-
         def linear_branch(g, half):
             for t in range(PACK):
                 feature_tile(g, half, t)
@@ -196,18 +198,18 @@ def tile_list_telematics_claim_scoring_kernel(
         def round_h(g, half, engine, lo=0, hi=P):
             if lo == 0:
                 h_bf[g, half] = held([P, W * PACK], BF16, "h_bf%d%d" % (g, half))
-            dst = h_bf[g, half][:].rearrange("p (c i t) -> p c t i", i=4, t=PACK)
-            src = h[g, half].rearrange("p t (c i) -> p c t i", i=4)
-            rounded(engine, dst[:, lo:hi], src[:, lo:hi])
+            dst = h_bf[g, half][:].rearrange("p (j t) -> p j t", t=PACK)[:, 4 * lo : 4 * hi]
+            src = h[g, half].rearrange("p t j -> p j t")[:, 4 * lo : 4 * hi]
+            rounded(engine, dst, src)
 
-        def store_h(g, half):
-            nc.sync.dma_start(feature_rows(g)[:, :, half * W : (half + 1) * W], h[g, half])
+        def store_h(g, half, lo, hi):
+            nc.sync.dma_start(feature_rows(g)[:, lo:hi, half * W : (half + 1) * W], h[g, half][:, lo:hi, :])
 
         def h_plane(g, half):
             return h_scales[:, g * S + half * W : g * S + (half + 1) * W]
 
-        def quantize_h(g, half):
-            h_codes[g, half] = held([P, W], U32, "h_codes%d%d" % (g, half))
+        def quantize_h(g, half, tag=None):
+            h_codes[g, half] = held([P, W], U32, "h_codes%d%d" % (g, half), tag)
             nc.vector.quantize_mx(out=h_codes[g, half][:].bitcast(FP8X4), scales=h_plane(g, half), in_=h_bf[g, half][:])
             nc.sync.dma_start(
                 out_2[g].rearrange("p m t -> p (m t)").bitcast(I32)[:, half * W : (half + 1) * W],
@@ -234,17 +236,11 @@ def tile_list_telematics_claim_scoring_kernel(
                 nc.vector.tensor_tensor(claims[:], rate[:], expo[:, i, cols], ALU.mult)
                 nc.sync.dma_start(out_0[i * P : (i + 1) * P, cols], claims[:])
 
-        def load_w3():
-            nc.sync.dma_start(
-                w3_codes[:].rearrange("p (a c) -> p a c", a=2),
-                w3_words.rearrange("a p c i -> p a (c i)").bitcast(I32),
-            )
-
         def store_scales():
-            for q in (0, 2, 1, 3):
+            for r in range(4):
                 nc.sync.dma_start(
-                    out_3[:, 4 * q : 4 * q + 4, :].rearrange("g r j -> r g j").bitcast(I32),
-                    h_scales[32 * q : 32 * q + 4, :].bitcast(I32).rearrange("p (g j) -> p g j", g=2),
+                    out_3[:, r:16:4, :].rearrange("g q j -> q g j").bitcast(I32),
+                    h_scales[r:P:32, :].bitcast(I32).rearrange("p (g j) -> p g j", g=2),
                 )
 
         for half in range(2):
@@ -258,27 +254,30 @@ def tile_list_telematics_claim_scoring_kernel(
         quantize_w2(0, 0)
         round_w2(0, 1, "vector", "slot_q")
         quantize_w2(0, 1)
-        w3_codes = held([P, 2 * N], I32, "w3_codes", "slot_b")
-        load_w3()
-        expo = held([P, 2, S], F32, "expo", "slot_t0")
+        expo = held([P, 2, S], F32, "expo", "slot_w0")
         nc.sync.dma_start(expo[:], exposure.rearrange("(i p) j -> p i j", p=P))
         gelu_branch(1, 0)
-        gelu_branch(1, 1)
         round_w2(1, 0, "vector")
-        first_group_pair(0)
+        linear_branch(0, 0)
         quantize_w2(1, 0)
-        round_w2(1, 1, "scalar")
+        gelu_branch(1, 1)
+        round_w2(1, 1, "vector")
+        linear_branch(0, 1)
         quantize_w2(1, 1)
-        first_group_pair(1)
         round_h(0, 0, "scalar")
-        linear_branch(1, 0)
         round_h(0, 1, "scalar")
+        linear_branch(1, 0)
         quantize_h(0, 0)
         round_h(1, 0, "scalar")
-        linear_branch(1, 1)
+        feature_tile(1, 1, 0)
+        feature_tile(1, 1, 1)
+        store_h(1, 1, 0, 2)
         quantize_h(0, 1)
-        quantize_h(1, 0)
+        feature_tile(1, 1, 2)
+        feature_tile(1, 1, 3)
+        store_h(1, 1, 2, 4)
         round_h(1, 1, "vector")
+        quantize_h(1, 0)
         quantize_h(1, 1)
         head(0)
         store_scales()

@@ -1,6 +1,7 @@
 from contextlib import ExitStack
 
 import concourse.mybir as mybir
+from concourse.masks import make_identity
 
 K, T, S, H, N = 1024, 4096, 1024, 1024, 256
 FLOPS = 2 * (2 * K * H * S + H * N * S)
@@ -32,7 +33,7 @@ def tile_list_telematics_claim_scoring_kernel(
     with ExitStack() as ctx:
         lists = ctx.enter_context(tc.tile_pool(name="lists", bufs=1))
         keep = ctx.enter_context(tc.tile_pool(name="keep", bufs=1))
-        psum = ctx.enter_context(tc.psum_pool(name="psum", bufs=8))
+        psum = ctx.enter_context(tc.psum_pool(name="psum", bufs=1))
 
         def held(shape, dtype, name, tag=None):
             return keep.tile(shape, dtype, name=name, tag=tag or name, align_bytes=64)
@@ -61,17 +62,22 @@ def tile_list_telematics_claim_scoring_kernel(
             nc.sync.dma_start(table[a][:], tab_words[a].rearrange("p t i -> p (t i)").bitcast(I32))
 
         load_table(0)
-        gains = held([P, 2, PACK], F32, "gains")
-        nc.sync.dma_start(gains[:], gain.rearrange("(g p t) -> p g t", g=2, t=PACK))
-        w3_codes = held([P, 2 * N], I32, "w3_codes")
-        nc.sync.dma_start(
-            w3_codes[:].rearrange("p (a c) -> p a c", a=2),
-            w3_words.rearrange("a p c i -> p a (c i)").bitcast(I32),
-        )
 
         nc.vector.memset(tab_rows[0:R0, :].bitcast(I32), 0)
         nc.vector.memset(w1_rows[0:R0, :].bitcast(I32), 0)
         nc.vector.memset(planes[:].bitcast(I32), 0)
+
+        vec_rows = held([P, PASS], F32, "vec_rows")
+        nc.gpsimd.memset(vec_rows[:], 0.0)
+        nc.sync.dma_start(vec_rows[0:2, :], b1.rearrange("(g c) -> g c", g=2))
+        nc.sync.dma_start(vec_rows[2:4, :], gain.rearrange("(g c) -> g c", g=2))
+        identity = held([P, P], F32, "identity")
+        make_identity(nc, identity[:])
+        turned = psum.tile([P, PACK, P], F32, name="turned", tag="bank7")
+        for t in range(PACK):
+            nc.tensor.transpose(turned[:, t, :], vec_rows[:, t:PASS:PACK], identity[:])
+        vecs = held([P, PACK, 4], F32, "vecs")
+        nc.scalar.copy(vecs[:], turned[:, :, 0:4])
 
         picked_rows = held([P, S], U8, "picked_rows", "slot_t1")
         nc.vector.tensor_copy(picked_rows[:], tab_rows[:].indirect(offsets[:]))
@@ -86,8 +92,6 @@ def tile_list_telematics_claim_scoring_kernel(
                 rows[R0 + 8 * q : R0 + 8 * q + 8, :].bitcast(I32),
             )
         load_table(1)
-        bias = held([P, 2, PACK], F32, "bias")
-        nc.scalar.dma_start(bias[:], b1.rearrange("(g p t) -> p g t", g=2, t=PACK))
 
         w1_codes = held([P, 2 * 2 * H], U8, "w1_codes", "slot_c")
         for a in range(2):
@@ -126,8 +130,8 @@ def tile_list_telematics_claim_scoring_kernel(
         def round_w2(g, a, engine, tag=None, lo=0, hi=P):
             if lo == 0:
                 w2_bf[g, a] = held([P, PASS * PACK], BF16, "w2_bf%d%d" % (g, a), tag)
-            dst = w2_bf[g, a][:].rearrange("p (t m j) -> p m t j", t=PACK, j=PACK)
-            src = w2_raw[g, a][:].rearrange("p j (m t) -> p m t j", t=PACK)
+            dst = w2_bf[g, a][:].rearrange("p (t m j) -> p m j t", t=PACK, j=PACK)
+            src = w2_raw[g, a][:].rearrange("p j (m t) -> p m j t", t=PACK)
             rounded(engine, dst[:, lo:hi], src[:, lo:hi])
 
         def quantize_w2(g, a, tag=None):
@@ -146,7 +150,7 @@ def tile_list_telematics_claim_scoring_kernel(
         def w1_pass(g, half, t, a):
             col = g * PASS + t * P
             if a == 0:
-                pre[g, half, t] = psum.tile([P, W], F32, name="acc")
+                pre[g, half, t] = psum.tile([P, W], F32, name="pre%d%d%d" % (g, half, t), tag="bank%d" % (4 * half + t))
             nc.tensor.matmul_mx(
                 out=pre[g, half, t][:],
                 lhsT=w1_codes[:, 2 * (a * H + col) : 2 * (a * H + col + P)].bitcast(FP4X4),
@@ -159,7 +163,7 @@ def tile_list_telematics_claim_scoring_kernel(
 
         def gelu(g, half, t):
             act[g, half, t] = held([P, W], F32, "act%d%d%d" % (g, half, t))
-            nc.scalar.activation(act[g, half, t][:], pre[g, half, t][:], ACT.Gelu_apprx_tanh, bias=bias[:, g, t : t + 1])
+            nc.scalar.activation(act[g, half, t][:], pre[g, half, t][:], ACT.Gelu_apprx_tanh, bias=vecs[:, t, g : g + 1])
 
         def gelu_branch(g, half):
             for t in range(PACK):
@@ -172,7 +176,7 @@ def tile_list_telematics_claim_scoring_kernel(
             h[1, half] = held([P, PACK, W], F32, "h1%d" % half)[:]
 
         def feature_tile(g, half, t):
-            acc = psum.tile([P, W], F32, name="acc")
+            acc = psum.tile([P, W], F32, name="lin%d%d%d" % (g, half, t), tag="bank%d" % (4 * ((g + half + 1) % 2) + t))
             for a in range(2):
                 nc.tensor.matmul_mx(
                     out=acc[:],
@@ -184,7 +188,7 @@ def tile_list_telematics_claim_scoring_kernel(
                     stop=(a == 1),
                 )
             nc.vector.scalar_tensor_tensor(
-                h[g, half][:, t, :], act[g, half, t][:], gains[:, g, t : t + 1], acc[:], ALU.mult, ALU.add
+                h[g, half][:, t, :], act[g, half, t][:], vecs[:, t, 2 + g : 3 + g], acc[:], ALU.mult, ALU.add
             )
 
         def feature_rows(g):
@@ -198,8 +202,8 @@ def tile_list_telematics_claim_scoring_kernel(
         def round_h(g, half, engine, lo=0, hi=P):
             if lo == 0:
                 h_bf[g, half] = held([P, W * PACK], BF16, "h_bf%d%d" % (g, half))
-            dst = h_bf[g, half][:].rearrange("p (j t) -> p j t", t=PACK)[:, 4 * lo : 4 * hi]
-            src = h[g, half].rearrange("p t j -> p j t")[:, 4 * lo : 4 * hi]
+            dst = h_bf[g, half][:].rearrange("p (c i t) -> p c t i", i=4, t=PACK)[:, lo:hi]
+            src = h[g, half].rearrange("p t (c i) -> p c t i", i=4)[:, lo:hi]
             rounded(engine, dst, src)
 
         def store_h(g, half, lo, hi):
@@ -219,7 +223,7 @@ def tile_list_telematics_claim_scoring_kernel(
         def head(half):
             cols = slice(half * W, (half + 1) * W)
             for i in range(N // P):
-                acc = psum.tile([P, W], F32, name="acc")
+                acc = psum.tile([P, W], F32, name="logit%d%d" % (half, i), tag="bank%d" % (4 + 2 * half + i))
                 for g in range(2):
                     nc.tensor.matmul_mx(
                         out=acc[:],
@@ -254,30 +258,39 @@ def tile_list_telematics_claim_scoring_kernel(
         quantize_w2(0, 0)
         round_w2(0, 1, "vector", "slot_q")
         quantize_w2(0, 1)
-        expo = held([P, 2, S], F32, "expo", "slot_w0")
+        w3_codes = held([P, 2 * N], I32, "w3_codes", "slot_w0")
+        nc.sync.dma_start(
+            w3_codes[:].rearrange("p (a c) -> p a c", a=2),
+            w3_words.rearrange("a p c i -> p a (c i)").bitcast(I32),
+        )
+        expo = held([P, 2, S], F32, "expo", "slot_w1")
         nc.sync.dma_start(expo[:], exposure.rearrange("(i p) j -> p i j", p=P))
         gelu_branch(1, 0)
         round_w2(1, 0, "vector")
-        linear_branch(0, 0)
         quantize_w2(1, 0)
+        linear_branch(0, 0)
         gelu_branch(1, 1)
-        round_w2(1, 1, "vector")
-        linear_branch(0, 1)
-        quantize_w2(1, 1)
+        round_w2(1, 1, "vector", "act003")
+        feature_tile(0, 1, 0)
+        feature_tile(0, 1, 1)
+        quantize_w2(1, 1, "act011")
+        feature_tile(0, 1, 2)
+        feature_tile(0, 1, 3)
+        store_h(0, 1, 0, 4)
         round_h(0, 0, "scalar")
         round_h(0, 1, "scalar")
+        quantize_h(0, 0, "act013")
         linear_branch(1, 0)
-        quantize_h(0, 0)
         round_h(1, 0, "scalar")
         feature_tile(1, 1, 0)
         feature_tile(1, 1, 1)
         store_h(1, 1, 0, 2)
-        quantize_h(0, 1)
         feature_tile(1, 1, 2)
         feature_tile(1, 1, 3)
         store_h(1, 1, 2, 4)
+        quantize_h(0, 1, "act112")
         round_h(1, 1, "vector")
-        quantize_h(1, 0)
+        quantize_h(1, 0, "act113")
         quantize_h(1, 1)
         head(0)
         store_scales()

@@ -1,7 +1,6 @@
 from contextlib import ExitStack
 
 import concourse.mybir as mybir
-from concourse.masks import make_identity
 
 K, T, S, H, N = 1024, 4096, 1024, 1024, 256
 FLOPS = 2 * (2 * K * H * S + H * N * S)
@@ -32,11 +31,15 @@ def tile_list_telematics_claim_scoring_kernel(
     nc = tc.nc
     with ExitStack() as ctx:
         lists = ctx.enter_context(tc.tile_pool(name="lists", bufs=1))
+        stream = ctx.enter_context(tc.tile_pool(name="stream", bufs=1))
         keep = ctx.enter_context(tc.tile_pool(name="keep", bufs=1))
         psum = ctx.enter_context(tc.psum_pool(name="psum", bufs=1))
 
         def held(shape, dtype, name, tag=None):
             return keep.tile(shape, dtype, name=name, tag=tag or name, align_bytes=64)
+
+        def streamed(shape, dtype, name, kib):
+            return stream.tile(shape, dtype, name=name, offset=kib * 1024, align_bytes=64)
 
         offsets = lists.tile([P, S // 16], U16, name="offsets")
         nc.sync.dma_start(offsets[:], offs)
@@ -45,59 +48,55 @@ def tile_list_telematics_claim_scoring_kernel(
             return scales.rearrange("a q n -> q a n").bitcast(I32)
 
         tab_rows = held([P, T], U8, "tab_rows")
-        w1_rows = held([P, H], U8, "w1_rows", "slot_c")
+        w1_rows = held([P, H], U8, "w1_rows")
         rows = held([P, ROW], U8, "rows")
         planes = held([P, 2 * ROW], U8, "planes")
-        nc.sync.dma_start(tab_rows[R0:P, :].bitcast(I32), scale_rows(tab_scales))
         nc.sync.dma_start(w1_rows[R0:P, :].bitcast(I32), scale_rows(w1_scales))
+        nc.sync.dma_start(tab_rows[R0:P, :].bitcast(I32), scale_rows(tab_scales))
         nc.sync.dma_start(rows[R0:P, W30:ROW].bitcast(I32), scale_rows(w3_scales))
-        w1_raw = []
-        for a in range(2):
-            w1_raw.append(held([P, 2 * H], U8, "w1_raw%d" % a, "slot_w%d" % a))
-            nc.sync.dma_start(w1_raw[a][:].bitcast(I32), w1_words[a].bitcast(I32))
+        w1_raw = held([P, 2 * 2 * H], U8, "w1_raw")
+        nc.sync.dma_start(
+            w1_raw[:].bitcast(I32).rearrange("p (a c) -> p a c", a=2),
+            w1_words.rearrange("a p c -> p a c").bitcast(I32),
+        )
         table = []
 
         def load_table(a):
-            table.append(held([P, T], I32, "table%d" % a, "slot_t%d" % a))
+            table.append(streamed([P, T], I32, "table%d" % a, 24 * a))
             nc.sync.dma_start(table[a][:], tab_words[a].rearrange("p t i -> p (t i)").bitcast(I32))
 
         load_table(0)
 
-        nc.vector.memset(tab_rows[0:R0, :].bitcast(I32), 0)
         nc.vector.memset(w1_rows[0:R0, :].bitcast(I32), 0)
+        nc.vector.memset(tab_rows[0:R0, :].bitcast(I32), 0)
         nc.vector.memset(planes[:].bitcast(I32), 0)
 
-        vec_rows = held([P, PASS], F32, "vec_rows")
-        nc.gpsimd.memset(vec_rows[:], 0.0)
-        nc.sync.dma_start(vec_rows[0:2, :], b1.rearrange("(g c) -> g c", g=2))
-        nc.sync.dma_start(vec_rows[2:4, :], gain.rearrange("(g c) -> g c", g=2))
-        identity = held([P, P], F32, "identity")
-        make_identity(nc, identity[:])
-        turned = psum.tile([P, PACK, P], F32, name="turned", tag="bank7")
-        for t in range(PACK):
-            nc.tensor.transpose(turned[:, t, :], vec_rows[:, t:PASS:PACK], identity[:])
-        vecs = held([P, PACK, 4], F32, "vecs")
-        nc.scalar.copy(vecs[:], turned[:, :, 0:4])
+        bias = held([P, 2, PACK], F32, "bias")
+        nc.scalar.dma_start(bias[:], b1.rearrange("(g p t) -> p g t", g=2, t=PACK))
+        gains = held([P, 2, PACK], F32, "gains")
+        nc.scalar.dma_start(gains[:], gain.rearrange("(g p t) -> p g t", g=2, t=PACK))
 
-        picked_rows = held([P, S], U8, "picked_rows", "slot_t1")
-        nc.vector.tensor_copy(picked_rows[:], tab_rows[:].indirect(offsets[:]))
+        picked_rows = streamed([P, S], U8, "picked_rows", 24)
         nc.vector.tensor_copy(
             rows[:, W10:W30].rearrange("p (g t m) -> p g t m", g=2, t=PACK),
             w1_rows[:].rearrange("p (g m t) -> p g t m", g=2, t=PACK),
         )
+        nc.vector.tensor_copy(picked_rows[:], tab_rows[:].indirect(offsets[:]))
         nc.vector.tensor_copy(rows[:, TAB0:W10].bitcast(I32), picked_rows[:].bitcast(I32))
         for q in (0, 2, 1, 3):
             nc.sync.dma_start(
                 planes[32 * q : 32 * q + 4, :].bitcast(I32).rearrange("p (a c) -> p a c", a=2),
                 rows[R0 + 8 * q : R0 + 8 * q + 8, :].bitcast(I32),
             )
+
         load_table(1)
 
-        w1_codes = held([P, 2 * 2 * H], U8, "w1_codes", "slot_c")
+        w1_codes = held([P, 2 * 2 * H], U8, "w1_codes")
         for a in range(2):
+            part = slice(a * 2 * H, (a + 1) * 2 * H)
             nc.vector.tensor_copy(
-                w1_codes[:, a * 2 * H : (a + 1) * 2 * H].bitcast(U16).rearrange("p (g t m) -> p g t m", g=2, t=PACK),
-                w1_raw[a][:].bitcast(U16).rearrange("p (g m t) -> p g t m", g=2, t=PACK),
+                w1_codes[:, part].bitcast(U16).rearrange("p (g t m) -> p g t m", g=2, t=PACK),
+                w1_raw[:, part].bitcast(U16).rearrange("p (g m t) -> p g t m", g=2, t=PACK),
             )
 
         picked = {}
@@ -110,29 +109,30 @@ def tile_list_telematics_claim_scoring_kernel(
                 )
 
         w2_raw = {}
-        for g, a, tag in ((0, 0, "slot_w0"), (0, 1, "slot_w1"), (1, 0, "slot_t0"), (1, 1, "slot_t1")):
-            w2_raw[g, a] = held([P, PACK, PASS], F32, "w2_raw%d%d" % (g, a), tag)
-            nc.sync.dma_start(
-                w2_raw[g, a][:],
-                w2[a * PASS : (a + 1) * PASS, g * PASS : (g + 1) * PASS].rearrange("(p j) c -> p j c", j=PACK),
-            )
+        for g in range(2):
+            for a in range(2):
+                w2_raw[g, a] = streamed([P, PACK, PASS], F32, "w2_raw%d%d" % (g, a), ((0, 8), (18, 38))[g][a])
+                nc.sync.dma_start(
+                    w2_raw[g, a][:],
+                    w2[a * PASS : (a + 1) * PASS, g * PASS : (g + 1) * PASS].rearrange("(p j) c -> p j c", j=PACK),
+                )
 
         w2_bf, w2_codes, w2_scales = {}, {}, {}
 
         def rounded(engine, dst, src):
             if engine == "vector":
                 nc.vector.tensor_copy(dst, src)
-            elif engine == "scalar":
-                nc.scalar.copy(dst, src)
             else:
-                nc.gpsimd.tensor_scalar(dst, src, 1.0, 0.0, ALU.mult, ALU.add)
+                nc.scalar.copy(dst, src)
 
-        def round_w2(g, a, engine, tag=None, lo=0, hi=P):
-            if lo == 0:
-                w2_bf[g, a] = held([P, PASS * PACK], BF16, "w2_bf%d%d" % (g, a), tag)
+        def round_w2(g, a, engine):
+            if (g, a) == (1, 1):
+                w2_bf[g, a] = held([P, PASS * PACK], BF16, "w2_bf11", "bias")
+            else:
+                w2_bf[g, a] = streamed([P, PASS * PACK], BF16, "w2_bf%d%d" % (g, a), 26 + 4 * (2 * g + a))
             dst = w2_bf[g, a][:].rearrange("p (t m j) -> p m j t", t=PACK, j=PACK)
             src = w2_raw[g, a][:].rearrange("p j (m t) -> p m j t", t=PACK)
-            rounded(engine, dst[:, lo:hi], src[:, lo:hi])
+            rounded(engine, dst, src)
 
         def quantize_w2(g, a, tag=None):
             w2_codes[g, a] = held([P, PASS], U32, "w2_codes%d%d" % (g, a), tag)
@@ -142,10 +142,9 @@ def tile_list_telematics_claim_scoring_kernel(
         def tab_plane(a, half):
             return planes[:, a * ROW + TAB0 + half * W : a * ROW + TAB0 + (half + 1) * W]
 
-        act, h, h_bf, h_codes = {}, {}, {}, {}
+        act, h, h_bf, pre = {}, {}, {}, {}
         h_scales = held([P, 2 * S], U8, "h_scales")
-
-        pre = {}
+        h_codes = [held([P, S], U32, "h_codes%d" % g) for g in range(2)]
 
         def w1_pass(g, half, t, a):
             col = g * PASS + t * P
@@ -163,20 +162,14 @@ def tile_list_telematics_claim_scoring_kernel(
 
         def gelu(g, half, t):
             act[g, half, t] = held([P, W], F32, "act%d%d%d" % (g, half, t))
-            nc.scalar.activation(act[g, half, t][:], pre[g, half, t][:], ACT.Gelu_apprx_tanh, bias=vecs[:, t, g : g + 1])
+            nc.scalar.activation(act[g, half, t][:], pre[g, half, t][:], ACT.Gelu_apprx_tanh, bias=bias[:, g, t : t + 1])
 
-        def gelu_branch(g, half):
-            for t in range(PACK):
-                w1_pass(g, half, t, 0)
-                w1_pass(g, half, t, 1)
-                gelu(g, half, t)
-
-        for half in range(2):
-            h[0, half] = held([P, PACK, W], F32, "h0%d" % half)[:]
-            h[1, half] = held([P, PACK, W], F32, "h1%d" % half)[:]
+        for g in range(2):
+            for half in range(2):
+                h[g, half] = held([P, PACK, W], F32, "h%d%d" % (g, half))
 
         def feature_tile(g, half, t):
-            acc = psum.tile([P, W], F32, name="lin%d%d%d" % (g, half, t), tag="bank%d" % (4 * ((g + half + 1) % 2) + t))
+            acc = psum.tile([P, W], F32, name="lin%d%d%d" % (g, half, t), tag="bank%d" % (4 * half + t))
             for a in range(2):
                 nc.tensor.matmul_mx(
                     out=acc[:],
@@ -188,57 +181,54 @@ def tile_list_telematics_claim_scoring_kernel(
                     stop=(a == 1),
                 )
             nc.vector.scalar_tensor_tensor(
-                h[g, half][:, t, :], act[g, half, t][:], vecs[:, t, 2 + g : 3 + g], acc[:], ALU.mult, ALU.add
+                h[g, half][:, t, :], act[g, half, t][:], gains[:, g, t : t + 1], acc[:], ALU.mult, ALU.add
             )
 
-        def feature_rows(g):
-            return out_1[g * PASS : (g + 1) * PASS, :].rearrange("(p t) j -> p t j", t=PACK)
+        def store_h(g, half):
+            rows_of_group = out_1[g * PASS : (g + 1) * PASS, :].rearrange("(p t) j -> p t j", t=PACK)
+            nc.sync.dma_start(rows_of_group[:, :, half * W : (half + 1) * W], h[g, half][:])
 
-        def linear_branch(g, half):
-            for t in range(PACK):
-                feature_tile(g, half, t)
-            nc.sync.dma_start(feature_rows(g)[:, :, half * W : (half + 1) * W], h[g, half])
-
-        def round_h(g, half, engine, lo=0, hi=P):
-            if lo == 0:
-                h_bf[g, half] = held([P, W * PACK], BF16, "h_bf%d%d" % (g, half))
-            dst = h_bf[g, half][:].rearrange("p (c i t) -> p c t i", i=4, t=PACK)[:, lo:hi]
-            src = h[g, half].rearrange("p t (c i) -> p c t i", i=4)[:, lo:hi]
+        def round_h(g, half, engine):
+            h_bf[g, half] = held([P, W * PACK], BF16, "h_bf%d%d" % (g, half))
+            dst = h_bf[g, half][:].rearrange("p (c i t) -> p c t i", i=4, t=PACK)
+            src = h[g, half][:].rearrange("p t (c i) -> p c t i", i=4)
             rounded(engine, dst, src)
-
-        def store_h(g, half, lo, hi):
-            nc.sync.dma_start(feature_rows(g)[:, lo:hi, half * W : (half + 1) * W], h[g, half][:, lo:hi, :])
 
         def h_plane(g, half):
             return h_scales[:, g * S + half * W : g * S + (half + 1) * W]
 
-        def quantize_h(g, half, tag=None):
-            h_codes[g, half] = held([P, W], U32, "h_codes%d%d" % (g, half), tag)
-            nc.vector.quantize_mx(out=h_codes[g, half][:].bitcast(FP8X4), scales=h_plane(g, half), in_=h_bf[g, half][:])
-            nc.sync.dma_start(
-                out_2[g].rearrange("p m t -> p (m t)").bitcast(I32)[:, half * W : (half + 1) * W],
-                h_codes[g, half][:].bitcast(I32),
+        def quantize_h(g, half):
+            nc.vector.quantize_mx(
+                out=h_codes[g][:, half * W : (half + 1) * W].bitcast(FP8X4), scales=h_plane(g, half), in_=h_bf[g, half][:]
             )
 
-        def head(half):
+        def store_codes(g, lo, hi):
+            nc.sync.dma_start(
+                out_2[g].rearrange("p m t -> p (m t)").bitcast(I32)[:, lo:hi], h_codes[g][:, lo:hi].bitcast(I32)
+            )
+
+        logit = {}
+
+        def head_pass(half, i, g):
+            if g == 0:
+                logit[half, i] = psum.tile([P, W], F32, name="logit%d%d" % (half, i), tag="bank%d" % (2 * half + i))
+            nc.tensor.matmul_mx(
+                out=logit[half, i][:],
+                lhsT=w3_codes[:, g * N + i * P : g * N + (i + 1) * P].bitcast(FP8X4),
+                lhsT_scale=planes[:, g * ROW + W30 + i * P : g * ROW + W30 + (i + 1) * P],
+                rhs=h_codes[g][:, half * W : (half + 1) * W].bitcast(FP8X4),
+                rhs_scale=h_plane(g, half),
+                start=(g == 0),
+                stop=(g == 1),
+            )
+
+        def claims_of(half, i):
             cols = slice(half * W, (half + 1) * W)
-            for i in range(N // P):
-                acc = psum.tile([P, W], F32, name="logit%d%d" % (half, i), tag="bank%d" % (4 + 2 * half + i))
-                for g in range(2):
-                    nc.tensor.matmul_mx(
-                        out=acc[:],
-                        lhsT=w3_codes[:, g * N + i * P : g * N + (i + 1) * P].bitcast(FP8X4),
-                        lhsT_scale=planes[:, g * ROW + W30 + i * P : g * ROW + W30 + (i + 1) * P],
-                        rhs=h_codes[g, half][:].bitcast(FP8X4),
-                        rhs_scale=h_plane(g, half),
-                        start=(g == 0),
-                        stop=(g == 1),
-                    )
-                rate = held([P, W], F32, "rate%d%d" % (half, i))
-                nc.scalar.activation(rate[:], acc[:], ACT.Exp)
-                claims = held([P, W], F32, "claims%d%d" % (half, i))
-                nc.vector.tensor_tensor(claims[:], rate[:], expo[:, i, cols], ALU.mult)
-                nc.sync.dma_start(out_0[i * P : (i + 1) * P, cols], claims[:])
+            rate = held([P, W], F32, "rate%d%d" % (half, i))
+            nc.scalar.activation(rate[:], logit[half, i][:], ACT.Exp)
+            claims = held([P, W], F32, "claims%d%d" % (half, i))
+            nc.vector.tensor_tensor(claims[:], rate[:], expo[:, i, cols], ALU.mult)
+            nc.sync.dma_start(out_0[i * P : (i + 1) * P, cols], claims[:])
 
         def store_scales():
             for r in range(4):
@@ -256,42 +246,55 @@ def tile_list_telematics_claim_scoring_kernel(
                 gelu(0, half, t)
         round_w2(0, 0, "vector")
         quantize_w2(0, 0)
-        round_w2(0, 1, "vector", "slot_q")
+        expo = streamed([P, 2, S], F32, "expo", 0)
+        nc.sync.dma_start(expo[:], exposure.rearrange("(i p) j -> p i j", p=P))
+        round_w2(0, 1, "vector")
         quantize_w2(0, 1)
-        w3_codes = held([P, 2 * N], I32, "w3_codes", "slot_w0")
+        w3_codes = streamed([P, 2 * N], I32, "w3_codes", 8)
         nc.sync.dma_start(
             w3_codes[:].rearrange("p (a c) -> p a c", a=2),
             w3_words.rearrange("a p c i -> p a (c i)").bitcast(I32),
         )
-        expo = held([P, 2, S], F32, "expo", "slot_w1")
-        nc.sync.dma_start(expo[:], exposure.rearrange("(i p) j -> p i j", p=P))
-        gelu_branch(1, 0)
+        for half in range(2):
+            for t in range(PACK):
+                w1_pass(1, half, t, 0)
+                w1_pass(1, half, t, 1)
+                gelu(1, half, t)
         round_w2(1, 0, "vector")
+        round_w2(1, 1, "scalar")
+        feature_tile(0, 0, 0)
         quantize_w2(1, 0)
-        linear_branch(0, 0)
-        gelu_branch(1, 1)
-        round_w2(1, 1, "vector", "act003")
-        feature_tile(0, 1, 0)
-        feature_tile(0, 1, 1)
-        quantize_w2(1, 1, "act011")
-        feature_tile(0, 1, 2)
-        feature_tile(0, 1, 3)
-        store_h(0, 1, 0, 4)
+        for t in range(1, PACK):
+            feature_tile(0, 0, t)
+        store_h(0, 0)
+        for t in range(PACK - 1):
+            feature_tile(0, 1, t)
+        quantize_w2(1, 1, "act012")
+        feature_tile(0, 1, PACK - 1)
+        store_h(0, 1)
         round_h(0, 0, "scalar")
         round_h(0, 1, "scalar")
-        quantize_h(0, 0, "act013")
-        linear_branch(1, 0)
+        for t in range(PACK):
+            feature_tile(1, 0, t)
+        store_h(1, 0)
         round_h(1, 0, "scalar")
-        feature_tile(1, 1, 0)
-        feature_tile(1, 1, 1)
-        store_h(1, 1, 0, 2)
-        feature_tile(1, 1, 2)
-        feature_tile(1, 1, 3)
-        store_h(1, 1, 2, 4)
-        quantize_h(0, 1, "act112")
+        for t in range(PACK):
+            feature_tile(1, 1, t)
+        store_h(1, 1)
+        quantize_h(0, 0)
+        quantize_h(0, 1)
+        store_codes(0, 0, S)
         round_h(1, 1, "vector")
-        quantize_h(1, 0, "act113")
+        quantize_h(1, 0)
+        store_codes(1, 0, W)
         quantize_h(1, 1)
-        head(0)
-        store_scales()
-        head(1)
+        store_codes(1, W, S)
+        for half in range(2):
+            for i in range(N // P):
+                head_pass(half, i, 0)
+        for half in range(2):
+            for i in range(N // P):
+                head_pass(half, i, 1)
+                claims_of(half, i)
+            if half == 0:
+                store_scales()

@@ -21,7 +21,7 @@ PACK = 4
 PASS = P * PACK
 W = 512
 R0 = 96
-TAB0, W10, W30, ROW = 0, S, S + H, S + H + N
+TAB0, W10, W30, ROW = 0, W, W + H, W + H + N
 
 
 def tile_list_telematics_claim_scoring_kernel(
@@ -39,7 +39,7 @@ def tile_list_telematics_claim_scoring_kernel(
             return keep.tile(shape, dtype, name=name, tag=tag or name, align_bytes=64)
 
         def streamed(shape, dtype, name, kib):
-            return stream.tile(shape, dtype, name=name, offset=kib * 1024, align_bytes=64)
+            return stream.tile(shape, dtype, name=name, offset=int(kib * 1024), align_bytes=64)
 
         offsets = lists.tile([P, S // 16], U16, name="offsets")
         nc.sync.dma_start(offsets[:], offs)
@@ -51,6 +51,7 @@ def tile_list_telematics_claim_scoring_kernel(
         w1_rows = held([P, H], U8, "w1_rows")
         rows = held([P, ROW], U8, "rows")
         planes = held([P, 2 * ROW], U8, "planes")
+        second_planes = held([P, 2 * W], U8, "second_planes")
         nc.sync.dma_start(w1_rows[R0:P, :].bitcast(I32), scale_rows(w1_scales))
         nc.sync.dma_start(tab_rows[R0:P, :].bitcast(I32), scale_rows(tab_scales))
         nc.sync.dma_start(rows[R0:P, W30:ROW].bitcast(I32), scale_rows(w3_scales))
@@ -62,7 +63,7 @@ def tile_list_telematics_claim_scoring_kernel(
         table = []
 
         def load_table(a):
-            table.append(streamed([P, T], I32, "table%d" % a, 24 * a))
+            table.append(streamed([P, T], I32, "table%d" % a, 25 * a))
             nc.sync.dma_start(table[a][:], tab_words[a].rearrange("p t i -> p (t i)").bitcast(I32))
 
         load_table(0)
@@ -70,26 +71,38 @@ def tile_list_telematics_claim_scoring_kernel(
         nc.vector.memset(w1_rows[0:R0, :].bitcast(I32), 0)
         nc.vector.memset(tab_rows[0:R0, :].bitcast(I32), 0)
         nc.vector.memset(planes[:].bitcast(I32), 0)
+        nc.vector.memset(second_planes[:].bitcast(I32), 0)
 
-        bias = held([P, 2, PACK], F32, "bias")
-        nc.scalar.dma_start(bias[:], b1.rearrange("(g p t) -> p g t", g=2, t=PACK))
-        gains = held([P, 2, PACK], F32, "gains")
-        nc.scalar.dma_start(gains[:], gain.rearrange("(g p t) -> p g t", g=2, t=PACK))
+        bias = [held([P, PACK], F32, "bias0")]
+        nc.scalar.dma_start(bias[0][:], b1[0:PASS].rearrange("(p t) -> p t", t=PACK))
 
-        picked_rows = streamed([P, S], U8, "picked_rows", 24)
         nc.vector.tensor_copy(
             rows[:, W10:W30].rearrange("p (g t m) -> p g t m", g=2, t=PACK),
             w1_rows[:].rearrange("p (g m t) -> p g t m", g=2, t=PACK),
         )
-        nc.vector.tensor_copy(picked_rows[:], tab_rows[:].indirect(offsets[:]))
-        nc.vector.tensor_copy(rows[:, TAB0:W10].bitcast(I32), picked_rows[:].bitcast(I32))
-        for q in (0, 2, 1, 3):
-            nc.sync.dma_start(
-                planes[32 * q : 32 * q + 4, :].bitcast(I32).rearrange("p (a c) -> p a c", a=2),
-                rows[R0 + 8 * q : R0 + 8 * q + 8, :].bitcast(I32),
-            )
 
+        def half_of_list(half):
+            return offsets[:, half * W // 16 : (half + 1) * W // 16]
+
+        def move_rows(dst, src):
+            for q in (0, 2, 1, 3):
+                nc.sync.dma_start(
+                    dst[32 * q : 32 * q + 4, :].bitcast(I32).rearrange("p (a c) -> p a c", a=2),
+                    src[R0 + 8 * q : R0 + 8 * q + 8, :].bitcast(I32),
+                )
+
+        first_rows = streamed([P, W], U8, "first_rows", 24.75)
+        nc.vector.tensor_copy(first_rows[:], tab_rows[:].indirect(half_of_list(0)))
+        nc.vector.tensor_copy(rows[:, TAB0:W10].bitcast(I32), first_rows[:].bitcast(I32))
+        move_rows(planes, rows)
+        bias.append(streamed([P, PACK], F32, "bias1", 24.875))
+        nc.scalar.dma_start(bias[1][:], b1[PASS:H].rearrange("(p t) -> p t", t=PACK))
+        gains = streamed([P, 2, PACK], F32, "gains", 24.9375)
+        nc.scalar.dma_start(gains[:], gain.rearrange("(g p t) -> p g t", g=2, t=PACK))
         load_table(1)
+        second_rows = streamed([P, W], U8, "second_rows", 24.375)
+        nc.vector.tensor_copy(second_rows[:], tab_rows[:].indirect(half_of_list(1)))
+        move_rows(second_planes, second_rows)
 
         w1_codes = held([P, 2 * 2 * H], U8, "w1_codes")
         for a in range(2):
@@ -105,17 +118,21 @@ def tile_list_telematics_claim_scoring_kernel(
                 picked[a, half] = held([P, W], U32, "picked%d%d" % (a, half))
                 nc.vector.tensor_copy(
                     picked[a, half][:],
-                    table[a][:].bitcast(U32).indirect(offsets[:, half * W // 16 : (half + 1) * W // 16]),
+                    table[a][:].bitcast(U32).indirect(half_of_list(half)),
                 )
 
         w2_raw = {}
-        for g in range(2):
-            for a in range(2):
-                w2_raw[g, a] = streamed([P, PACK, PASS], F32, "w2_raw%d%d" % (g, a), ((0, 8), (18, 38))[g][a])
-                nc.sync.dma_start(
-                    w2_raw[g, a][:],
-                    w2[a * PASS : (a + 1) * PASS, g * PASS : (g + 1) * PASS].rearrange("(p j) c -> p j c", j=PACK),
-                )
+
+        def load_w2(g, a):
+            w2_raw[g, a] = streamed([P, PACK, PASS], F32, "w2_raw%d%d" % (g, a), ((0, 8), (25, 0))[g][a])
+            nc.sync.dma_start(
+                w2_raw[g, a][:],
+                w2[a * PASS : (a + 1) * PASS, g * PASS : (g + 1) * PASS].rearrange("(p j) c -> p j c", j=PACK),
+            )
+
+        load_w2(0, 0)
+        load_w2(0, 1)
+        load_w2(1, 0)
 
         w2_bf, w2_codes, w2_scales = {}, {}, {}
 
@@ -127,9 +144,9 @@ def tile_list_telematics_claim_scoring_kernel(
 
         def round_w2(g, a, engine):
             if (g, a) == (1, 1):
-                w2_bf[g, a] = held([P, PASS * PACK], BF16, "w2_bf11", "bias")
+                w2_bf[g, a] = held([P, PASS * PACK], BF16, "w2_bf11", "bias0")
             else:
-                w2_bf[g, a] = streamed([P, PASS * PACK], BF16, "w2_bf%d%d" % (g, a), 26 + 4 * (2 * g + a))
+                w2_bf[g, a] = streamed([P, PASS * PACK], BF16, "w2_bf%d%d" % (g, a), (33, 37, 48)[2 * g + a])
             dst = w2_bf[g, a][:].rearrange("p (t m j) -> p m j t", t=PACK, j=PACK)
             src = w2_raw[g, a][:].rearrange("p j (m t) -> p m j t", t=PACK)
             rounded(engine, dst, src)
@@ -140,16 +157,18 @@ def tile_list_telematics_claim_scoring_kernel(
             nc.vector.quantize_mx(out=w2_codes[g, a][:].bitcast(FP8X4), scales=w2_scales[g, a][:], in_=w2_bf[g, a][:])
 
         def tab_plane(a, half):
-            return planes[:, a * ROW + TAB0 + half * W : a * ROW + TAB0 + (half + 1) * W]
+            if half == 0:
+                return planes[:, a * ROW + TAB0 : a * ROW + W10]
+            return second_planes[:, a * W : (a + 1) * W]
 
         act, h, h_bf, pre = {}, {}, {}, {}
         h_scales = held([P, 2 * S], U8, "h_scales")
         h_codes = [held([P, S], U32, "h_codes%d" % g) for g in range(2)]
 
-        def w1_pass(g, half, t, a):
+        def w1_pass(g, half, t, a, side):
             col = g * PASS + t * P
             if a == 0:
-                pre[g, half, t] = psum.tile([P, W], F32, name="pre%d%d%d" % (g, half, t), tag="bank%d" % (4 * half + t))
+                pre[g, half, t] = psum.tile([P, W], F32, name="pre%d%d%d" % (g, half, t), tag="bank%d" % (4 * side + t))
             nc.tensor.matmul_mx(
                 out=pre[g, half, t][:],
                 lhsT=w1_codes[:, 2 * (a * H + col) : 2 * (a * H + col + P)].bitcast(FP4X4),
@@ -161,32 +180,42 @@ def tile_list_telematics_claim_scoring_kernel(
             )
 
         def gelu(g, half, t):
-            act[g, half, t] = held([P, W], F32, "act%d%d%d" % (g, half, t))
-            nc.scalar.activation(act[g, half, t][:], pre[g, half, t][:], ACT.Gelu_apprx_tanh, bias=bias[:, g, t : t + 1])
+            if (g, half) == (1, 1):
+                act[g, half, t] = streamed([P, W], F32, "act11%d" % t, 2 * t)
+            else:
+                act[g, half, t] = held([P, W], F32, "act%d%d%d" % (g, half, t))
+            nc.scalar.activation(act[g, half, t][:], pre[g, half, t][:], ACT.Gelu_apprx_tanh, bias=bias[g][:, t : t + 1])
 
         for g in range(2):
             for half in range(2):
-                h[g, half] = held([P, PACK, W], F32, "h%d%d" % (g, half))
+                if (g, half) != (0, 0):
+                    h[g, half] = held([P, PACK, W], F32, "h%d%d" % (g, half))
 
-        def feature_tile(g, half, t):
-            acc = psum.tile([P, W], F32, name="lin%d%d%d" % (g, half, t), tag="bank%d" % (4 * half + t))
-            for a in range(2):
+        def feature_tile(g, half, t, side):
+            acc = psum.tile([P, W], F32, name="lin%d%d%d" % (g, half, t), tag="bank%d" % (4 * side + t))
+            for a in (1, 0):
                 nc.tensor.matmul_mx(
                     out=acc[:],
                     lhsT=w2_codes[g, a][:, t * P : (t + 1) * P].bitcast(FP8X4),
                     lhsT_scale=w2_scales[g, a][:, t * P : (t + 1) * P],
                     rhs=picked[a, half][:].bitcast(FP8X4),
                     rhs_scale=tab_plane(a, half),
-                    start=(a == 0),
-                    stop=(a == 1),
+                    start=(a == 1),
+                    stop=(a == 0),
                 )
             nc.vector.scalar_tensor_tensor(
                 h[g, half][:, t, :], act[g, half, t][:], gains[:, g, t : t + 1], acc[:], ALU.mult, ALU.add
             )
 
-        def store_h(g, half):
+        def store_h(g, half, lo, hi):
             rows_of_group = out_1[g * PASS : (g + 1) * PASS, :].rearrange("(p t) j -> p t j", t=PACK)
-            nc.sync.dma_start(rows_of_group[:, :, half * W : (half + 1) * W], h[g, half][:])
+            nc.sync.dma_start(rows_of_group[:, lo:hi, half * W : (half + 1) * W], h[g, half][:, lo:hi, :])
+
+        def linear_unit(g, half, side):
+            for lo in range(0, PACK, 2):
+                feature_tile(g, half, lo, side)
+                feature_tile(g, half, lo + 1, side)
+                store_h(g, half, lo, lo + 2)
 
         def round_h(g, half, engine):
             h_bf[g, half] = held([P, W * PACK], BF16, "h_bf%d%d" % (g, half))
@@ -211,7 +240,7 @@ def tile_list_telematics_claim_scoring_kernel(
 
         def head_pass(half, i, g):
             if g == 0:
-                logit[half, i] = psum.tile([P, W], F32, name="logit%d%d" % (half, i), tag="bank%d" % (2 * half + i))
+                logit[half, i] = psum.tile([P, W], F32, name="logit%d%d" % (half, i), tag="bank%d" % (4 + 2 * half + i))
             nc.tensor.matmul_mx(
                 out=logit[half, i][:],
                 lhsT=w3_codes[:, g * N + i * P : g * N + (i + 1) * P].bitcast(FP8X4),
@@ -237,58 +266,54 @@ def tile_list_telematics_claim_scoring_kernel(
                     h_scales[r:P:32, :].bitcast(I32).rearrange("p (g j) -> p g j", g=2),
                 )
 
-        for half in range(2):
+        def gelu_unit(g, half, side):
             for t in range(PACK):
-                w1_pass(0, half, t, 0)
-        for half in range(2):
+                w1_pass(g, half, t, 0, side)
+                w1_pass(g, half, t, 1, side)
+                gelu(g, half, t)
+
+        for g in range(2):
             for t in range(PACK):
-                w1_pass(0, half, t, 1)
-                gelu(0, half, t)
+                w1_pass(g, 0, t, 0, g)
+        for g in range(2):
+            for t in range(PACK):
+                w1_pass(g, 0, t, 1, g)
+                gelu(g, 0, t)
         round_w2(0, 0, "vector")
+        load_w2(1, 1)
         quantize_w2(0, 0)
-        expo = streamed([P, 2, S], F32, "expo", 0)
-        nc.sync.dma_start(expo[:], exposure.rearrange("(i p) j -> p i j", p=P))
-        round_w2(0, 1, "vector")
-        quantize_w2(0, 1)
-        w3_codes = streamed([P, 2 * N], I32, "w3_codes", 8)
+        w3_codes = streamed([P, 2 * N], I32, "w3_codes", 33)
         nc.sync.dma_start(
             w3_codes[:].rearrange("p (a c) -> p a c", a=2),
             w3_words.rearrange("a p c i -> p a (c i)").bitcast(I32),
         )
-        for half in range(2):
-            for t in range(PACK):
-                w1_pass(1, half, t, 0)
-                w1_pass(1, half, t, 1)
-                gelu(1, half, t)
+        round_w2(0, 1, "vector")
+        quantize_w2(0, 1)
+        expo = streamed([P, 2, S], F32, "expo", 8)
+        nc.sync.dma_start(expo[:], exposure.rearrange("(i p) j -> p i j", p=P))
+        gelu_unit(0, 1, 0)
         round_w2(1, 0, "vector")
         round_w2(1, 1, "scalar")
-        feature_tile(0, 0, 0)
+        gelu_unit(1, 1, 1)
         quantize_w2(1, 0)
-        for t in range(1, PACK):
-            feature_tile(0, 0, t)
-        store_h(0, 0)
-        for t in range(PACK - 1):
-            feature_tile(0, 1, t)
-        quantize_w2(1, 1, "act012")
-        feature_tile(0, 1, PACK - 1)
-        store_h(0, 1)
+        h[0, 0] = streamed([P, PACK, W], F32, "h00", 48)
+        for t in range(PACK):
+            feature_tile(0, 0, t, 0)
+        store_h(0, 0, 0, PACK)
+        quantize_w2(1, 1, "act003")
+        linear_unit(0, 1, 0)
         round_h(0, 0, "scalar")
         round_h(0, 1, "scalar")
-        for t in range(PACK):
-            feature_tile(1, 0, t)
-        store_h(1, 0)
+        linear_unit(1, 0, 1)
         round_h(1, 0, "scalar")
-        for t in range(PACK):
-            feature_tile(1, 1, t)
-        store_h(1, 1)
+        linear_unit(1, 1, 0)
         quantize_h(0, 0)
+        round_h(1, 1, "vector")
         quantize_h(0, 1)
         store_codes(0, 0, S)
-        round_h(1, 1, "vector")
         quantize_h(1, 0)
-        store_codes(1, 0, W)
         quantize_h(1, 1)
-        store_codes(1, W, S)
+        store_codes(1, 0, S)
         for half in range(2):
             for i in range(N // P):
                 head_pass(half, i, 0)

@@ -63,7 +63,7 @@ def tile_list_telematics_claim_scoring_kernel(
         table = []
 
         def load_table(a):
-            table.append(streamed([P, T], I32, "table%d" % a, 25 * a))
+            table.append(streamed([P, T], I32, "table%d" % a, 1 + 24 * a))
             nc.sync.dma_start(table[a][:], tab_words[a].rearrange("p t i -> p (t i)").bitcast(I32))
 
         load_table(0)
@@ -73,8 +73,8 @@ def tile_list_telematics_claim_scoring_kernel(
         nc.vector.memset(planes[:].bitcast(I32), 0)
         nc.vector.memset(second_planes[:].bitcast(I32), 0)
 
-        bias = [held([P, PACK], F32, "bias0")]
-        nc.scalar.dma_start(bias[0][:], b1[0:PASS].rearrange("(p t) -> p t", t=PACK))
+        bias = held([P, 2, PACK], F32, "bias")
+        nc.scalar.dma_start(bias[:], b1.rearrange("(g p t) -> p g t", g=2, t=PACK))
 
         nc.vector.tensor_copy(
             rows[:, W10:W30].rearrange("p (g t m) -> p g t m", g=2, t=PACK),
@@ -86,7 +86,8 @@ def tile_list_telematics_claim_scoring_kernel(
 
         def move_rows(dst, src):
             for q in (0, 2, 1, 3):
-                nc.sync.dma_start(
+                queue = nc.sync if q < 2 else nc.scalar
+                queue.dma_start(
                     dst[32 * q : 32 * q + 4, :].bitcast(I32).rearrange("p (a c) -> p a c", a=2),
                     src[R0 + 8 * q : R0 + 8 * q + 8, :].bitcast(I32),
                 )
@@ -95,10 +96,6 @@ def tile_list_telematics_claim_scoring_kernel(
         nc.vector.tensor_copy(first_rows[:], tab_rows[:].indirect(half_of_list(0)))
         nc.vector.tensor_copy(rows[:, TAB0:W10].bitcast(I32), first_rows[:].bitcast(I32))
         move_rows(planes, rows)
-        bias.append(streamed([P, PACK], F32, "bias1", 24.875))
-        nc.scalar.dma_start(bias[1][:], b1[PASS:H].rearrange("(p t) -> p t", t=PACK))
-        gains = streamed([P, 2, PACK], F32, "gains", 24.9375)
-        nc.scalar.dma_start(gains[:], gain.rearrange("(g p t) -> p g t", g=2, t=PACK))
         load_table(1)
         second_rows = streamed([P, W], U8, "second_rows", 24.375)
         nc.vector.tensor_copy(second_rows[:], tab_rows[:].indirect(half_of_list(1)))
@@ -132,6 +129,8 @@ def tile_list_telematics_claim_scoring_kernel(
 
         load_w2(0, 0)
         load_w2(0, 1)
+        gains = streamed([P, 2, PACK], F32, "gains", 16.0625)
+        nc.sync.dma_start(gains[:], gain.rearrange("(g p t) -> p g t", g=2, t=PACK))
         load_w2(1, 0)
 
         w2_bf, w2_codes, w2_scales = {}, {}, {}
@@ -144,7 +143,7 @@ def tile_list_telematics_claim_scoring_kernel(
 
         def round_w2(g, a, engine):
             if (g, a) == (1, 1):
-                w2_bf[g, a] = held([P, PASS * PACK], BF16, "w2_bf11", "bias0")
+                w2_bf[g, a] = held([P, PASS * PACK], BF16, "w2_bf11")
             else:
                 w2_bf[g, a] = streamed([P, PASS * PACK], BF16, "w2_bf%d%d" % (g, a), (33, 37, 48)[2 * g + a])
             dst = w2_bf[g, a][:].rearrange("p (t m j) -> p m j t", t=PACK, j=PACK)
@@ -184,7 +183,7 @@ def tile_list_telematics_claim_scoring_kernel(
                 act[g, half, t] = streamed([P, W], F32, "act11%d" % t, 2 * t)
             else:
                 act[g, half, t] = held([P, W], F32, "act%d%d%d" % (g, half, t))
-            nc.scalar.activation(act[g, half, t][:], pre[g, half, t][:], ACT.Gelu_apprx_tanh, bias=bias[g][:, t : t + 1])
+            nc.scalar.activation(act[g, half, t][:], pre[g, half, t][:], ACT.Gelu_apprx_tanh, bias=bias[:, g, t : t + 1])
 
         for g in range(2):
             for half in range(2):

@@ -1,6 +1,7 @@
 from contextlib import ExitStack
 
 import concourse.mybir as mybir
+from concourse.masks import make_identity
 
 K, T, S, H, N = 1024, 4096, 1024, 1024, 256
 FLOPS = 2 * (2 * K * H * S + H * N * S)
@@ -60,6 +61,10 @@ def tile_list_telematics_claim_scoring_kernel(
             w1_raw[:].bitcast(I32).rearrange("p (a c) -> p a c", a=2),
             w1_words.rearrange("a p c -> p a c").bitcast(I32),
         )
+        vec_rows = held([P, PASS], F32, "vec_rows")
+        nc.gpsimd.memset(vec_rows[:], 0.0)
+        nc.sync.dma_start(vec_rows[0:2, :], b1.rearrange("(g c) -> g c", g=2))
+        nc.sync.dma_start(vec_rows[2:4, :], gain.rearrange("(g c) -> g c", g=2))
         table = []
 
         def load_table(a):
@@ -73,8 +78,6 @@ def tile_list_telematics_claim_scoring_kernel(
         nc.vector.memset(planes[:].bitcast(I32), 0)
         nc.vector.memset(second_planes[:].bitcast(I32), 0)
 
-        bias = held([P, 2, PACK], F32, "bias")
-        nc.scalar.dma_start(bias[:], b1.rearrange("(g p t) -> p g t", g=2, t=PACK))
 
         nc.vector.tensor_copy(
             rows[:, W10:W30].rearrange("p (g t m) -> p g t m", g=2, t=PACK),
@@ -109,6 +112,14 @@ def tile_list_telematics_claim_scoring_kernel(
                 w1_raw[:, part].bitcast(U16).rearrange("p (g m t) -> p g t m", g=2, t=PACK),
             )
 
+        identity = held([P, P], F32, "identity", "w1_raw")
+        make_identity(nc, identity[:])
+        turned = psum.tile([P, PACK, P], F32, name="turned", tag="bank7")
+        for t in range(PACK):
+            nc.tensor.transpose(turned[:, t, :], vec_rows[:, t:PASS:PACK], identity[:])
+        vecs = held([P, PACK, 4], F32, "vecs")
+        nc.scalar.copy(vecs[:], turned[:, :, 0:4])
+
         picked = {}
         for a in range(2):
             for half in range(2):
@@ -129,8 +140,6 @@ def tile_list_telematics_claim_scoring_kernel(
 
         load_w2(0, 0)
         load_w2(0, 1)
-        gains = streamed([P, 2, PACK], F32, "gains", 16.0625)
-        nc.sync.dma_start(gains[:], gain.rearrange("(g p t) -> p g t", g=2, t=PACK))
         load_w2(1, 0)
 
         w2_bf, w2_codes, w2_scales = {}, {}, {}
@@ -164,10 +173,10 @@ def tile_list_telematics_claim_scoring_kernel(
         h_scales = held([P, 2 * S], U8, "h_scales")
         h_codes = [held([P, S], U32, "h_codes%d" % g) for g in range(2)]
 
-        def w1_pass(g, half, t, a, side):
+        def w1_pass(g, half, t, a, bank):
             col = g * PASS + t * P
             if a == 0:
-                pre[g, half, t] = psum.tile([P, W], F32, name="pre%d%d%d" % (g, half, t), tag="bank%d" % (4 * side + t))
+                pre[g, half, t] = psum.tile([P, W], F32, name="pre%d%d%d" % (g, half, t), tag="bank%d" % bank)
             nc.tensor.matmul_mx(
                 out=pre[g, half, t][:],
                 lhsT=w1_codes[:, 2 * (a * H + col) : 2 * (a * H + col + P)].bitcast(FP4X4),
@@ -183,15 +192,15 @@ def tile_list_telematics_claim_scoring_kernel(
                 act[g, half, t] = streamed([P, W], F32, "act11%d" % t, 2 * t)
             else:
                 act[g, half, t] = held([P, W], F32, "act%d%d%d" % (g, half, t))
-            nc.scalar.activation(act[g, half, t][:], pre[g, half, t][:], ACT.Gelu_apprx_tanh, bias=bias[:, g, t : t + 1])
+            nc.scalar.activation(act[g, half, t][:], pre[g, half, t][:], ACT.Gelu_apprx_tanh, bias=vecs[:, t, g : g + 1])
 
         for g in range(2):
             for half in range(2):
                 if (g, half) != (0, 0):
                     h[g, half] = held([P, PACK, W], F32, "h%d%d" % (g, half))
 
-        def feature_tile(g, half, t, side):
-            acc = psum.tile([P, W], F32, name="lin%d%d%d" % (g, half, t), tag="bank%d" % (4 * side + t))
+        def feature_tile(g, half, t, bank):
+            acc = psum.tile([P, W], F32, name="lin%d%d%d" % (g, half, t), tag="bank%d" % bank)
             for a in (1, 0):
                 nc.tensor.matmul_mx(
                     out=acc[:],
@@ -203,18 +212,20 @@ def tile_list_telematics_claim_scoring_kernel(
                     stop=(a == 0),
                 )
             nc.vector.scalar_tensor_tensor(
-                h[g, half][:, t, :], act[g, half, t][:], gains[:, g, t : t + 1], acc[:], ALU.mult, ALU.add
+                h[g, half][:, t, :], act[g, half, t][:], vecs[:, t, 2 + g : 3 + g], acc[:], ALU.mult, ALU.add
             )
 
         def store_h(g, half, lo, hi):
             rows_of_group = out_1[g * PASS : (g + 1) * PASS, :].rearrange("(p t) j -> p t j", t=PACK)
             nc.sync.dma_start(rows_of_group[:, lo:hi, half * W : (half + 1) * W], h[g, half][:, lo:hi, :])
 
-        def linear_unit(g, half, side):
-            for lo in range(0, PACK, 2):
-                feature_tile(g, half, lo, side)
-                feature_tile(g, half, lo + 1, side)
-                store_h(g, half, lo, lo + 2)
+        def feature_pair(g, half, lo, bank):
+            feature_tile(g, half, lo, bank)
+            feature_tile(g, half, lo + 1, bank + 1)
+
+        def stored_pair(g, half, lo, bank):
+            feature_pair(g, half, lo, bank)
+            store_h(g, half, lo, lo + 2)
 
         def round_h(g, half, engine):
             h_bf[g, half] = held([P, W * PACK], BF16, "h_bf%d%d" % (g, half))
@@ -239,7 +250,7 @@ def tile_list_telematics_claim_scoring_kernel(
 
         def head_pass(half, i, g):
             if g == 0:
-                logit[half, i] = psum.tile([P, W], F32, name="logit%d%d" % (half, i), tag="bank%d" % (4 + 2 * half + i))
+                logit[half, i] = psum.tile([P, W], F32, name="logit%d%d" % (half, i), tag="bank%d" % (2 + 4 * half + i))
             nc.tensor.matmul_mx(
                 out=logit[half, i][:],
                 lhsT=w3_codes[:, g * N + i * P : g * N + (i + 1) * P].bitcast(FP8X4),
@@ -265,18 +276,17 @@ def tile_list_telematics_claim_scoring_kernel(
                     h_scales[r:P:32, :].bitcast(I32).rearrange("p (g j) -> p g j", g=2),
                 )
 
-        def gelu_unit(g, half, side):
-            for t in range(PACK):
-                w1_pass(g, half, t, 0, side)
-                w1_pass(g, half, t, 1, side)
-                gelu(g, half, t)
+        def w1_pair(g, half, lo, bank):
+            for t in (lo, lo + 1):
+                w1_pass(g, half, t, 0, bank + t - lo)
+                w1_pass(g, half, t, 1, bank + t - lo)
 
         for g in range(2):
             for t in range(PACK):
-                w1_pass(g, 0, t, 0, g)
+                w1_pass(g, 0, t, 0, PACK * g + t)
         for g in range(2):
             for t in range(PACK):
-                w1_pass(g, 0, t, 1, g)
+                w1_pass(g, 0, t, 1, PACK * g + t)
                 gelu(g, 0, t)
         round_w2(0, 0, "vector")
         load_w2(1, 1)
@@ -290,22 +300,31 @@ def tile_list_telematics_claim_scoring_kernel(
         quantize_w2(0, 1)
         expo = streamed([P, 2, S], F32, "expo", 8)
         nc.sync.dma_start(expo[:], exposure.rearrange("(i p) j -> p i j", p=P))
-        gelu_unit(0, 1, 0)
+        w1_pair(0, 1, 0, 0)
+        w1_pair(0, 1, 2, 2)
+        for t in range(PACK):
+            gelu(0, 1, t)
+        w1_pair(1, 1, 0, 4)
         round_w2(1, 0, "vector")
         round_w2(1, 1, "scalar")
-        gelu_unit(1, 1, 1)
         quantize_w2(1, 0)
         h[0, 0] = streamed([P, PACK, W], F32, "h00", 48)
-        for t in range(PACK):
-            feature_tile(0, 0, t, 0)
+        feature_pair(0, 0, 0, 6)
+        feature_pair(0, 0, 2, 0)
         store_h(0, 0, 0, PACK)
-        quantize_w2(1, 1, "act003")
-        linear_unit(0, 1, 0)
+        stored_pair(0, 1, 0, 2)
+        quantize_w2(1, 1, "act011")
+        stored_pair(0, 1, 2, 6)
+        w1_pair(1, 1, 2, 0)
+        for t in range(PACK):
+            gelu(1, 1, t)
         round_h(0, 0, "scalar")
         round_h(0, 1, "scalar")
-        linear_unit(1, 0, 1)
+        stored_pair(1, 0, 0, 2)
+        stored_pair(1, 0, 2, 6)
         round_h(1, 0, "scalar")
-        linear_unit(1, 1, 0)
+        stored_pair(1, 1, 0, 4)
+        stored_pair(1, 1, 2, 0)
         quantize_h(0, 0)
         round_h(1, 1, "vector")
         quantize_h(0, 1)

@@ -48,7 +48,7 @@ def tile_list_telematics_claim_scoring_kernel(
         def scale_rows(scales):
             return scales.rearrange("a q n -> q a n").bitcast(I32)
 
-        tab_rows = held([P, T], U8, "tab_rows")
+        tab_rows = streamed([P, T], U8, "tab_rows", 60)
         w1_rows = held([P, H], U8, "w1_rows")
         rows = held([P, ROW], U8, "rows")
         planes = held([P, 2 * ROW], U8, "planes")
@@ -100,19 +100,20 @@ def tile_list_telematics_claim_scoring_kernel(
         nc.vector.tensor_copy(rows[:, TAB0:W10].bitcast(I32), first_rows[:].bitcast(I32))
         move_rows(planes, rows)
         load_table(1)
-        second_rows = streamed([P, W], U8, "second_rows", 24.375)
-        nc.vector.tensor_copy(second_rows[:], tab_rows[:].indirect(half_of_list(1)))
-        move_rows(second_planes, second_rows)
 
-        w1_codes = held([P, 2 * 2 * H], U8, "w1_codes")
-        for a in range(2):
-            part = slice(a * 2 * H, (a + 1) * 2 * H)
+        w1_codes = {}
+
+        def deal_w1(g, a, codes):
+            w1_codes[g, a] = codes
+            words = w1_raw[:, 2 * (a * H + g * PASS) : 2 * (a * H + (g + 1) * PASS)]
             nc.vector.tensor_copy(
-                w1_codes[:, part].bitcast(U16).rearrange("p (g t m) -> p g t m", g=2, t=PACK),
-                w1_raw[:, part].bitcast(U16).rearrange("p (g m t) -> p g t m", g=2, t=PACK),
+                codes[:].bitcast(U16).rearrange("p (t m) -> p t m", t=PACK),
+                words.bitcast(U16).rearrange("p (m t) -> p t m", t=PACK),
             )
 
-        identity = held([P, P], F32, "identity", "w1_raw")
+        deal_w1(0, 0, held([P, 2 * PASS], U8, "w1_codes00"))
+
+        identity = held([P, P], F32, "identity")
         make_identity(nc, identity[:])
         turned = psum.tile([P, PACK, P], F32, name="turned", tag="bank7")
         for t in range(PACK):
@@ -121,24 +122,31 @@ def tile_list_telematics_claim_scoring_kernel(
         nc.scalar.copy(vecs[:], turned[:, :, 0:4])
 
         picked = {}
-        for a in range(2):
+
+        def pick(a):
             for half in range(2):
                 picked[a, half] = held([P, W], U32, "picked%d%d" % (a, half))
-                nc.vector.tensor_copy(
-                    picked[a, half][:],
-                    table[a][:].bitcast(U32).indirect(half_of_list(half)),
-                )
+                nc.vector.tensor_copy(picked[a, half][:], table[a][:].bitcast(U32).indirect(half_of_list(half)))
 
         w2_raw = {}
 
         def load_w2(g, a):
-            w2_raw[g, a] = streamed([P, PACK, PASS], F32, "w2_raw%d%d" % (g, a), ((0, 8), (25, 0))[g][a])
+            w2_raw[g, a] = streamed([P, PACK, PASS], F32, "w2_raw%d%d" % (g, a), ((8, 62), (25, 8))[g][a])
             nc.sync.dma_start(
                 w2_raw[g, a][:],
                 w2[a * PASS : (a + 1) * PASS, g * PASS : (g + 1) * PASS].rearrange("(p j) c -> p j c", j=PACK),
             )
 
+        pick(0)
         load_w2(0, 0)
+        deal_w1(0, 1, streamed([P, 2 * PASS], U8, "w1_codes01", 1))
+        deal_w1(1, 1, streamed([P, 2 * PASS], U8, "w1_codes11", 2))
+        second_rows = streamed([P, W], U8, "second_rows", 3)
+        nc.vector.tensor_copy(second_rows[:], tab_rows[:].indirect(half_of_list(1)))
+        move_rows(second_planes, second_rows)
+        deal_w1(1, 0, streamed([P, 2 * PASS], U8, "w1_codes10", 4))
+        pick(1)
+
         load_w2(0, 1)
         load_w2(1, 0)
 
@@ -154,7 +162,7 @@ def tile_list_telematics_claim_scoring_kernel(
             if (g, a) == (1, 1):
                 w2_bf[g, a] = held([P, PASS * PACK], BF16, "w2_bf11")
             else:
-                w2_bf[g, a] = streamed([P, PASS * PACK], BF16, "w2_bf%d%d" % (g, a), (33, 37, 48)[2 * g + a])
+                w2_bf[g, a] = streamed([P, PASS * PACK], BF16, "w2_bf%d%d" % (g, a), (33, 37, 72)[2 * g + a])
             dst = w2_bf[g, a][:].rearrange("p (t m j) -> p m j t", t=PACK, j=PACK)
             src = w2_raw[g, a][:].rearrange("p j (m t) -> p m j t", t=PACK)
             rounded(engine, dst, src)
@@ -179,7 +187,7 @@ def tile_list_telematics_claim_scoring_kernel(
                 pre[g, half, t] = psum.tile([P, W], F32, name="pre%d%d%d" % (g, half, t), tag="bank%d" % bank)
             nc.tensor.matmul_mx(
                 out=pre[g, half, t][:],
-                lhsT=w1_codes[:, 2 * (a * H + col) : 2 * (a * H + col + P)].bitcast(FP4X4),
+                lhsT=w1_codes[g, a][:, 2 * t * P : 2 * (t + 1) * P].bitcast(FP4X4),
                 lhsT_scale=planes[:, a * ROW + W10 + col : a * ROW + W10 + col + P],
                 rhs=picked[a, half][:].bitcast(FP8X4),
                 rhs_scale=tab_plane(a, half),
@@ -189,7 +197,7 @@ def tile_list_telematics_claim_scoring_kernel(
 
         def gelu(g, half, t):
             if (g, half) == (1, 1):
-                act[g, half, t] = streamed([P, W], F32, "act11%d" % t, 2 * t)
+                act[g, half, t] = streamed([P, W], F32, "act11%d" % t, 8 + 2 * t)
             else:
                 act[g, half, t] = held([P, W], F32, "act%d%d%d" % (g, half, t))
             nc.scalar.activation(act[g, half, t][:], pre[g, half, t][:], ACT.Gelu_apprx_tanh, bias=vecs[:, t, g : g + 1])
@@ -298,7 +306,7 @@ def tile_list_telematics_claim_scoring_kernel(
         )
         round_w2(0, 1, "vector")
         quantize_w2(0, 1)
-        expo = streamed([P, 2, S], F32, "expo", 8)
+        expo = streamed([P, 2, S], F32, "expo", 62)
         nc.sync.dma_start(expo[:], exposure.rearrange("(i p) j -> p i j", p=P))
         w1_pair(0, 1, 0, 0)
         w1_pair(0, 1, 2, 2)
@@ -308,7 +316,7 @@ def tile_list_telematics_claim_scoring_kernel(
         round_w2(1, 0, "vector")
         round_w2(1, 1, "scalar")
         quantize_w2(1, 0)
-        h[0, 0] = streamed([P, PACK, W], F32, "h00", 48)
+        h[0, 0] = streamed([P, PACK, W], F32, "h00", 72)
         feature_pair(0, 0, 0, 6)
         feature_pair(0, 0, 2, 0)
         store_h(0, 0, 0, PACK)

@@ -255,6 +255,7 @@ def tile_list_telematics_claim_scoring_kernel(
             )
 
         logit = {}
+        claims = [held([P, N // P, W], F32, "claims%d" % half) for half in range(2)]
 
         def head_pass(half, i, g):
             if g == 0:
@@ -273,9 +274,11 @@ def tile_list_telematics_claim_scoring_kernel(
             cols = slice(half * W, (half + 1) * W)
             rate = held([P, W], F32, "rate%d%d" % (half, i))
             nc.scalar.activation(rate[:], logit[half, i][:], ACT.Exp)
-            claims = held([P, W], F32, "claims%d%d" % (half, i))
-            nc.vector.tensor_tensor(claims[:], rate[:], expo[:, i, cols], ALU.mult)
-            nc.sync.dma_start(out_0[i * P : (i + 1) * P, cols], claims[:])
+            nc.vector.tensor_tensor(claims[half][:, i, :], rate[:], expo[:, i, cols], ALU.mult)
+
+        def store_claims(half, lo, hi):
+            cols = slice(half * W, (half + 1) * W)
+            nc.sync.dma_start(out_0.rearrange("(i p) j -> p i j", p=P)[:, lo:hi, cols], claims[half][:, lo:hi, :])
 
         def store_scales():
             for r in range(4):
@@ -330,16 +333,18 @@ def tile_list_telematics_claim_scoring_kernel(
         round_h(0, 1, "scalar")
         stored_pair(1, 0, 0, 2)
         stored_pair(1, 0, 2, 6)
+        quantize_h(0, 0)
+        store_codes(0, 0, W)
         round_h(1, 0, "scalar")
         stored_pair(1, 1, 0, 4)
         stored_pair(1, 1, 2, 0)
-        quantize_h(0, 0)
-        round_h(1, 1, "vector")
         quantize_h(0, 1)
-        store_codes(0, 0, S)
+        store_codes(0, W, S)
+        round_h(1, 1, "vector")
         quantize_h(1, 0)
         quantize_h(1, 1)
         store_codes(1, 0, S)
+        store_scales()
         for half in range(2):
             for i in range(N // P):
                 head_pass(half, i, 0)
@@ -347,5 +352,4 @@ def tile_list_telematics_claim_scoring_kernel(
             for i in range(N // P):
                 head_pass(half, i, 1)
                 claims_of(half, i)
-            if half == 0:
-                store_scales()
+                store_claims(half, i, i + 1)

@@ -196,7 +196,7 @@ def tile_list_telematics_claim_scoring_kernel(
             )
 
         def gelu(g, half, t):
-            if (g, half) == (1, 1):
+            if (g, half) == (1, 1) and t >= 2:
                 act[g, half, t] = streamed([P, W], F32, "act11%d" % t, 8 + 2 * t)
             else:
                 act[g, half, t] = held([P, W], F32, "act%d%d%d" % (g, half, t))
@@ -316,19 +316,22 @@ def tile_list_telematics_claim_scoring_kernel(
         for t in range(PACK):
             gelu(0, 1, t)
         w1_pair(1, 1, 0, 4)
+        gelu(1, 1, 0)
+        gelu(1, 1, 1)
         round_w2(1, 0, "vector")
         round_w2(1, 1, "scalar")
+        h[0, 0] = streamed([P, PACK, W], F32, "h00", 25)
+        feature_tile(0, 0, 0, 6)
         quantize_w2(1, 0)
-        h[0, 0] = streamed([P, PACK, W], F32, "h00", 72)
-        feature_pair(0, 0, 0, 6)
+        feature_tile(0, 0, 1, 7)
         feature_pair(0, 0, 2, 0)
         store_h(0, 0, 0, PACK)
         stored_pair(0, 1, 0, 2)
-        quantize_w2(1, 1, "act011")
+        quantize_w2(1, 1, "act010")
         stored_pair(0, 1, 2, 6)
         w1_pair(1, 1, 2, 0)
-        for t in range(PACK):
-            gelu(1, 1, t)
+        gelu(1, 1, 2)
+        gelu(1, 1, 3)
         round_h(0, 0, "scalar")
         round_h(0, 1, "scalar")
         stored_pair(1, 0, 0, 2)

@@ -69,7 +69,7 @@ def tile_list_telematics_claim_scoring_kernel(
 
         def load_table(a):
             table.append(streamed([P, T], I32, "table%d" % a, 1 + 24 * a))
-            nc.sync.dma_start(table[a][:], tab_words[a].rearrange("p t i -> p (t i)").bitcast(I32))
+            nc.sync.dma_start(table[a][:], tab_words[a].rearrange("p t i -> p (t i)").bitcast(I32), max_dma_last_dim=2048)
 
         load_table(0)
 

@@ -22,7 +22,8 @@ PACK = 4
 PASS = P * PACK
 W = 512
 R0 = 96
-TAB0, W10, W30, ROW = 0, W, W + H, W + H + N
+TAB0, W10, ROW = 0, W, W + H
+W30, LATE_ROW = W, W + N
 
 
 def tile_list_telematics_claim_scoring_kernel(
@@ -52,10 +53,10 @@ def tile_list_telematics_claim_scoring_kernel(
         w1_rows = held([P, H], U8, "w1_rows")
         rows = held([P, ROW], U8, "rows")
         planes = held([P, 2 * ROW], U8, "planes")
-        second_planes = held([P, 2 * W], U8, "second_planes")
+        late_rows = held([P, LATE_ROW], U8, "late_rows")
+        second_planes = held([P, 2 * LATE_ROW], U8, "second_planes")
         nc.sync.dma_start(w1_rows[R0:P, :].bitcast(I32), scale_rows(w1_scales))
         nc.sync.dma_start(tab_rows[R0:P, :].bitcast(I32), scale_rows(tab_scales))
-        nc.sync.dma_start(rows[R0:P, W30:ROW].bitcast(I32), scale_rows(w3_scales))
         w1_raw = held([P, 2 * 2 * H], U8, "w1_raw")
         nc.sync.dma_start(
             w1_raw[:].bitcast(I32).rearrange("p (a c) -> p a c", a=2),
@@ -63,8 +64,8 @@ def tile_list_telematics_claim_scoring_kernel(
         )
         vec_rows = held([P, PASS], F32, "vec_rows")
         nc.gpsimd.memset(vec_rows[:], 0.0)
-        nc.sync.dma_start(vec_rows[0:2, :], b1.rearrange("(g c) -> g c", g=2))
-        nc.sync.dma_start(vec_rows[2:4, :], gain.rearrange("(g c) -> g c", g=2))
+        nc.sync.dma_start(vec_rows[4:6, :], b1.rearrange("(g c) -> g c", g=2))
+        nc.sync.dma_start(vec_rows[6:8, :], gain.rearrange("(g c) -> g c", g=2))
         table = []
 
         def load_table(a):
@@ -72,6 +73,7 @@ def tile_list_telematics_claim_scoring_kernel(
             nc.sync.dma_start(table[a][:], tab_words[a].rearrange("p t i -> p (t i)").bitcast(I32), max_dma_last_dim=2048)
 
         load_table(0)
+        nc.sync.dma_start(late_rows[R0:P, W30:LATE_ROW].bitcast(I32), scale_rows(w3_scales))
 
         nc.vector.memset(w1_rows[0:R0, :].bitcast(I32), 0)
         nc.vector.memset(tab_rows[0:R0, :].bitcast(I32), 0)
@@ -80,7 +82,7 @@ def tile_list_telematics_claim_scoring_kernel(
 
 
         nc.vector.tensor_copy(
-            rows[:, W10:W30].rearrange("p (g t m) -> p g t m", g=2, t=PACK),
+            rows[:, W10:ROW].rearrange("p (g t m) -> p g t m", g=2, t=PACK),
             w1_rows[:].rearrange("p (g m t) -> p g t m", g=2, t=PACK),
         )
 
@@ -112,6 +114,7 @@ def tile_list_telematics_claim_scoring_kernel(
             )
 
         deal_w1(0, 0, held([P, 2 * PASS], U8, "w1_codes00"))
+        deal_w1(0, 1, held([P, 2 * PASS], U8, "w1_codes01"))
 
         identity = held([P, P], F32, "identity")
         make_identity(nc, identity[:])
@@ -119,7 +122,7 @@ def tile_list_telematics_claim_scoring_kernel(
         for t in range(PACK):
             nc.tensor.transpose(turned[:, t, :], vec_rows[:, t:PASS:PACK], identity[:])
         vecs = held([P, PACK, 4], F32, "vecs")
-        nc.scalar.copy(vecs[:], turned[:, :, 0:4])
+        nc.scalar.copy(vecs[:], turned[:, :, 4:8])
 
         picked = {}
 
@@ -139,11 +142,11 @@ def tile_list_telematics_claim_scoring_kernel(
 
         pick(0)
         load_w2(0, 0)
-        deal_w1(0, 1, streamed([P, 2 * PASS], U8, "w1_codes01", 1))
         deal_w1(1, 1, streamed([P, 2 * PASS], U8, "w1_codes11", 2))
         second_rows = streamed([P, W], U8, "second_rows", 3)
         nc.vector.tensor_copy(second_rows[:], tab_rows[:].indirect(half_of_list(1)))
-        move_rows(second_planes, second_rows)
+        nc.vector.tensor_copy(late_rows[R0:P, 0:W].bitcast(I32), second_rows[R0:P, :].bitcast(I32))
+        move_rows(second_planes, late_rows)
         deal_w1(1, 0, streamed([P, 2 * PASS], U8, "w1_codes10", 4))
         pick(1)
 
@@ -175,7 +178,7 @@ def tile_list_telematics_claim_scoring_kernel(
         def tab_plane(a, half):
             if half == 0:
                 return planes[:, a * ROW + TAB0 : a * ROW + W10]
-            return second_planes[:, a * W : (a + 1) * W]
+            return second_planes[:, a * LATE_ROW : a * LATE_ROW + W]
 
         act, h, h_bf, pre = {}, {}, {}, {}
         h_scales = held([P, 2 * S], U8, "h_scales")
@@ -235,18 +238,21 @@ def tile_list_telematics_claim_scoring_kernel(
             feature_pair(g, half, lo, bank)
             store_h(g, half, lo, lo + 2)
 
-        def round_h(g, half, engine):
-            h_bf[g, half] = held([P, W * PACK], BF16, "h_bf%d%d" % (g, half))
-            dst = h_bf[g, half][:].rearrange("p (c i t) -> p c t i", i=4, t=PACK)
-            src = h[g, half][:].rearrange("p t (c i) -> p c t i", i=4)
+        def round_h(g, half, engine, lo=0, hi=W):
+            if (g, half) not in h_bf:
+                h_bf[g, half] = held([P, W * PACK], BF16, "h_bf%d%d" % (g, half))
+            dst = h_bf[g, half][:, lo * PACK : hi * PACK].rearrange("p (c i t) -> p c t i", i=4, t=PACK)
+            src = h[g, half][:, :, lo:hi].rearrange("p t (c i) -> p c t i", i=4)
             rounded(engine, dst, src)
 
         def h_plane(g, half):
             return h_scales[:, g * S + half * W : g * S + (half + 1) * W]
 
-        def quantize_h(g, half):
+        def quantize_h(g, half, lo=0, hi=W):
             nc.vector.quantize_mx(
-                out=h_codes[g][:, half * W : (half + 1) * W].bitcast(FP8X4), scales=h_plane(g, half), in_=h_bf[g, half][:]
+                out=h_codes[g][:, half * W + lo : half * W + hi].bitcast(FP8X4),
+                scales=h_plane(g, half)[:, lo:hi],
+                in_=h_bf[g, half][:, lo * PACK : hi * PACK],
             )
 
         def store_codes(g, lo, hi):
@@ -255,30 +261,27 @@ def tile_list_telematics_claim_scoring_kernel(
             )
 
         logit = {}
-        claims = [held([P, N // P, W], F32, "claims%d" % half) for half in range(2)]
 
-        def head_pass(half, i, g):
+        def head_pass(first, width, i, g, bank):
             if g == 0:
-                logit[half, i] = psum.tile([P, W], F32, name="logit%d%d" % (half, i), tag="bank%d" % (2 + 4 * half + i))
+                logit[first, i] = psum.tile([P, width], F32, name="logit%d_%d" % (first, i), tag="bank%d" % bank)
             nc.tensor.matmul_mx(
-                out=logit[half, i][:],
+                out=logit[first, i][:],
                 lhsT=w3_codes[:, g * N + i * P : g * N + (i + 1) * P].bitcast(FP8X4),
-                lhsT_scale=planes[:, g * ROW + W30 + i * P : g * ROW + W30 + (i + 1) * P],
-                rhs=h_codes[g][:, half * W : (half + 1) * W].bitcast(FP8X4),
-                rhs_scale=h_plane(g, half),
+                lhsT_scale=second_planes[:, g * LATE_ROW + W30 + i * P : g * LATE_ROW + W30 + (i + 1) * P],
+                rhs=h_codes[g][:, first : first + width].bitcast(FP8X4),
+                rhs_scale=h_scales[:, g * S + first : g * S + first + width],
                 start=(g == 0),
                 stop=(g == 1),
             )
 
-        def claims_of(half, i):
-            cols = slice(half * W, (half + 1) * W)
-            rate = held([P, W], F32, "rate%d%d" % (half, i))
-            nc.scalar.activation(rate[:], logit[half, i][:], ACT.Exp)
-            nc.vector.tensor_tensor(claims[half][:, i, :], rate[:], expo[:, i, cols], ALU.mult)
-
-        def store_claims(half, lo, hi):
-            cols = slice(half * W, (half + 1) * W)
-            nc.sync.dma_start(out_0.rearrange("(i p) j -> p i j", p=P)[:, lo:hi, cols], claims[half][:, lo:hi, :])
+        def claims_of(first, width, i):
+            cols = slice(first, first + width)
+            rate = held([P, width], F32, "rate%d_%d" % (first, i))
+            claims = held([P, width], F32, "claims%d_%d" % (first, i))
+            nc.scalar.activation(rate[:], logit[first, i][:], ACT.Exp)
+            nc.vector.tensor_tensor(claims[:], rate[:], expo[:, i, cols], ALU.mult)
+            nc.sync.dma_start(out_0[i * P : (i + 1) * P, cols], claims[:])
 
         def store_scales():
             for r in range(4):
@@ -338,21 +341,26 @@ def tile_list_telematics_claim_scoring_kernel(
         stored_pair(1, 0, 2, 6)
         quantize_h(0, 0)
         store_codes(0, 0, W)
-        round_h(1, 0, "scalar")
+        round_h(1, 0, "scalar", 0, 384)
+        round_h(1, 0, "vector", 384, W)
         stored_pair(1, 1, 0, 4)
         stored_pair(1, 1, 2, 0)
         quantize_h(0, 1)
         store_codes(0, W, S)
-        round_h(1, 1, "vector")
         quantize_h(1, 0)
-        quantize_h(1, 1)
-        store_codes(1, 0, S)
+        store_codes(1, 0, W)
+        round_h(1, 1, "vector", 0, W // 2)
+        round_h(1, 1, "vector", W // 2, W)
+        quantize_h(1, 1, 0, W // 2)
+        store_codes(1, W, W + W // 2)
+        quantize_h(1, 1, W // 2, W)
+        store_codes(1, W + W // 2, S)
         store_scales()
-        for half in range(2):
+        spans = ((0, W, 2), (W, W // 2, 6), (W + W // 2, W // 2, 4))
+        for first, width, bank in spans:
             for i in range(N // P):
-                head_pass(half, i, 0)
-        for half in range(2):
+                head_pass(first, width, i, 0, bank + i)
+        for first, width, bank in spans:
             for i in range(N // P):
-                head_pass(half, i, 1)
-                claims_of(half, i)
-                store_claims(half, i, i + 1)
+                head_pass(first, width, i, 1, bank + i)
+                claims_of(first, width, i)

@@ -275,13 +275,14 @@ def tile_list_telematics_claim_scoring_kernel(
                 stop=(g == 1),
             )
 
-        def claims_of(first, width, i):
-            cols = slice(first, first + width)
+        def claims_of(first, width, i, claims):
             rate = held([P, width], F32, "rate%d_%d" % (first, i))
-            claims = held([P, width], F32, "claims%d_%d" % (first, i))
             nc.scalar.activation(rate[:], logit[first, i][:], ACT.Exp)
-            nc.vector.tensor_tensor(claims[:], rate[:], expo[:, i, cols], ALU.mult)
-            nc.sync.dma_start(out_0[i * P : (i + 1) * P, cols], claims[:])
+            nc.vector.tensor_tensor(claims[:, i, :], rate[:], expo[:, i, first : first + width], ALU.mult)
+
+        def store_claims(first, width, lo, hi, claims):
+            dst = out_0.rearrange("(i p) j -> p i j", p=P)[:, lo:hi, first : first + width]
+            nc.sync.dma_start(dst, claims[:, lo:hi, :])
 
         def store_scales():
             for r in range(4):
@@ -361,6 +362,11 @@ def tile_list_telematics_claim_scoring_kernel(
             for i in range(N // P):
                 head_pass(first, width, i, 0, bank + i)
         for first, width, bank in spans:
+            claims = held([P, N // P, width], F32, "claims%d" % first)
             for i in range(N // P):
                 head_pass(first, width, i, 1, bank + i)
-                claims_of(first, width, i)
+                claims_of(first, width, i, claims)
+                if width == W:
+                    store_claims(first, width, i, i + 1, claims)
+            if width < W:
+                store_claims(first, width, 0, N // P, claims)

@@ -325,11 +325,9 @@ def tile_list_telematics_claim_scoring_kernel(
         round_w2(1, 0, "vector")
         round_w2(1, 1, "scalar")
         h[0, 0] = streamed([P, PACK, W], F32, "h00", 25)
-        feature_tile(0, 0, 0, 6)
+        stored_pair(0, 0, 0, 6)
         quantize_w2(1, 0)
-        feature_tile(0, 0, 1, 7)
-        feature_pair(0, 0, 2, 0)
-        store_h(0, 0, 0, PACK)
+        stored_pair(0, 0, 2, 0)
         stored_pair(0, 1, 0, 2)
         quantize_w2(1, 1, "act010")
         stored_pair(0, 1, 2, 6)

@@ -63,7 +63,7 @@ def tile_list_telematics_claim_scoring_kernel(
             w1_words.rearrange("a p c -> p a c").bitcast(I32),
         )
         vec_rows = held([P, PASS], F32, "vec_rows")
-        nc.gpsimd.memset(vec_rows[:], 0.0)
+        nc.vector.memset(vec_rows[:].bitcast(I32), 0)
         nc.sync.dma_start(vec_rows[4:6, :], b1.rearrange("(g c) -> g c", g=2))
         nc.sync.dma_start(vec_rows[6:8, :], gain.rearrange("(g c) -> g c", g=2))
         table = []
@@ -168,12 +168,22 @@ def tile_list_telematics_claim_scoring_kernel(
                 w2_bf[g, a] = streamed([P, PASS * PACK], BF16, "w2_bf%d%d" % (g, a), (33, 37, 72)[2 * g + a])
             dst = w2_bf[g, a][:].rearrange("p (t m j) -> p m j t", t=PACK, j=PACK)
             src = w2_raw[g, a][:].rearrange("p j (m t) -> p m j t", t=PACK)
-            rounded(engine, dst, src)
+            if g == 0:
+                for lo in (0, 2):
+                    rounded(engine, dst[:, :, :, lo : lo + 2], src[:, :, :, lo : lo + 2])
+            else:
+                rounded(engine, dst, src)
 
         def quantize_w2(g, a, tag=None):
             w2_codes[g, a] = held([P, PASS], U32, "w2_codes%d%d" % (g, a), tag)
             w2_scales[g, a] = held([P, PASS], U8, "w2_scales%d%d" % (g, a))
-            nc.vector.quantize_mx(out=w2_codes[g, a][:].bitcast(FP8X4), scales=w2_scales[g, a][:], in_=w2_bf[g, a][:])
+            step = PASS // 2 if g == 0 else PASS
+            for lo in range(0, PASS, step):
+                nc.vector.quantize_mx(
+                    out=w2_codes[g, a][:, lo : lo + step].bitcast(FP8X4),
+                    scales=w2_scales[g, a][:, lo : lo + step],
+                    in_=w2_bf[g, a][:, PACK * lo : PACK * (lo + step)],
+                )
 
         def tab_plane(a, half):
             if half == 0:
@@ -353,8 +363,8 @@ def tile_list_telematics_claim_scoring_kernel(
         quantize_h(1, 1, 0, W // 2)
         store_codes(1, W, W + W // 2)
         quantize_h(1, 1, W // 2, W)
-        store_codes(1, W + W // 2, S)
         store_scales()
+        store_codes(1, W + W // 2, S)
         spans = ((0, W, 2), (W, W // 2, 6), (W + W // 2, W // 2, 4))
         for first, width, bank in spans:
             for i in range(N // P):

@@ -161,29 +161,24 @@ def tile_list_telematics_claim_scoring_kernel(
             else:
                 nc.scalar.copy(dst, src)
 
-        def round_w2(g, a, engine):
+        def round_w2(g, a, first, second):
             if (g, a) == (1, 1):
                 w2_bf[g, a] = held([P, PASS * PACK], BF16, "w2_bf11")
             else:
                 w2_bf[g, a] = streamed([P, PASS * PACK], BF16, "w2_bf%d%d" % (g, a), (33, 37, 72)[2 * g + a])
             dst = w2_bf[g, a][:].rearrange("p (t m j) -> p m j t", t=PACK, j=PACK)
             src = w2_raw[g, a][:].rearrange("p j (m t) -> p m j t", t=PACK)
-            if g == 0:
-                for lo in (0, 2):
-                    rounded(engine, dst[:, :, :, lo : lo + 2], src[:, :, :, lo : lo + 2])
-            else:
-                rounded(engine, dst, src)
+            for lo, engine in ((0, first), (2, second)):
+                rounded(engine, dst[:, :, :, lo : lo + 2], src[:, :, :, lo : lo + 2])
 
-        def quantize_w2(g, a, tag=None):
-            w2_codes[g, a] = held([P, PASS], U32, "w2_codes%d%d" % (g, a), tag)
-            w2_scales[g, a] = held([P, PASS], U8, "w2_scales%d%d" % (g, a))
-            step = PASS // 2 if g == 0 else PASS
-            for lo in range(0, PASS, step):
-                nc.vector.quantize_mx(
-                    out=w2_codes[g, a][:, lo : lo + step].bitcast(FP8X4),
-                    scales=w2_scales[g, a][:, lo : lo + step],
-                    in_=w2_bf[g, a][:, PACK * lo : PACK * (lo + step)],
-                )
+        def quantize_w2(g, a, pair, tag=None):
+            w2_codes[g, a, pair] = held([P, PASS // 2], U32, "w2_codes%d%d%d" % (g, a, pair), tag)
+            w2_scales[g, a, pair] = held([P, PASS // 2], U8, "w2_scales%d%d%d" % (g, a, pair))
+            nc.vector.quantize_mx(
+                out=w2_codes[g, a, pair][:].bitcast(FP8X4),
+                scales=w2_scales[g, a, pair][:],
+                in_=w2_bf[g, a][:, pair * 2 * PASS : (pair + 1) * 2 * PASS],
+            )
 
         def tab_plane(a, half):
             if half == 0:
@@ -225,8 +220,8 @@ def tile_list_telematics_claim_scoring_kernel(
             for a in (1, 0):
                 nc.tensor.matmul_mx(
                     out=acc[:],
-                    lhsT=w2_codes[g, a][:, t * P : (t + 1) * P].bitcast(FP8X4),
-                    lhsT_scale=w2_scales[g, a][:, t * P : (t + 1) * P],
+                    lhsT=w2_codes[g, a, t // 2][:, t % 2 * P : (t % 2 + 1) * P].bitcast(FP8X4),
+                    lhsT_scale=w2_scales[g, a, t // 2][:, t % 2 * P : (t % 2 + 1) * P],
                     rhs=picked[a, half][:].bitcast(FP8X4),
                     rhs_scale=tab_plane(a, half),
                     start=(a == 1),
@@ -313,16 +308,18 @@ def tile_list_telematics_claim_scoring_kernel(
             for t in range(PACK):
                 w1_pass(g, 0, t, 1, PACK * g + t)
                 gelu(g, 0, t)
-        round_w2(0, 0, "vector")
+        round_w2(0, 0, "vector", "vector")
         load_w2(1, 1)
-        quantize_w2(0, 0)
+        quantize_w2(0, 0, 0)
+        quantize_w2(0, 0, 1)
         w3_codes = streamed([P, 2 * N], I32, "w3_codes", 33)
         nc.sync.dma_start(
             w3_codes[:].rearrange("p (a c) -> p a c", a=2),
             w3_words.rearrange("a p c i -> p a (c i)").bitcast(I32),
         )
-        round_w2(0, 1, "vector")
-        quantize_w2(0, 1)
+        round_w2(0, 1, "vector", "vector")
+        quantize_w2(0, 1, 0)
+        quantize_w2(0, 1, 1)
         expo = streamed([P, 2, S], F32, "expo", 62)
         nc.sync.dma_start(expo[:], exposure.rearrange("(i p) j -> p i j", p=P))
         w1_pair(0, 1, 0, 0)
@@ -332,15 +329,17 @@ def tile_list_telematics_claim_scoring_kernel(
         w1_pair(1, 1, 0, 4)
         gelu(1, 1, 0)
         gelu(1, 1, 1)
-        round_w2(1, 0, "vector")
-        round_w2(1, 1, "scalar")
+        round_w2(1, 0, "vector", "vector")
+        round_w2(1, 1, "scalar", "scalar")
         h[0, 0] = streamed([P, PACK, W], F32, "h00", 25)
+        quantize_w2(1, 0, 0)
         stored_pair(0, 0, 0, 6)
-        quantize_w2(1, 0)
+        quantize_w2(1, 0, 1)
         stored_pair(0, 0, 2, 0)
         stored_pair(0, 1, 0, 2)
-        quantize_w2(1, 1, "act010")
+        quantize_w2(1, 1, 0, "act010")
         stored_pair(0, 1, 2, 6)
+        quantize_w2(1, 1, 1, "act012")
         w1_pair(1, 1, 2, 0)
         gelu(1, 1, 2)
         gelu(1, 1, 3)

@@ -1,7 +1,6 @@
 from contextlib import ExitStack
 
 import concourse.mybir as mybir
-from concourse.masks import make_identity
 
 K, T, S, H, N = 1024, 4096, 1024, 1024, 256
 FLOPS = 2 * (2 * K * H * S + H * N * S)
@@ -62,10 +61,10 @@ def tile_list_telematics_claim_scoring_kernel(
             w1_raw[:].bitcast(I32).rearrange("p (a c) -> p a c", a=2),
             w1_words.rearrange("a p c -> p a c").bitcast(I32),
         )
-        vec_rows = held([P, PASS], F32, "vec_rows")
+        vec_rows = held([P, P], F32, "vec_rows")
         nc.vector.memset(vec_rows[:].bitcast(I32), 0)
-        nc.sync.dma_start(vec_rows[4:6, :], b1.rearrange("(g c) -> g c", g=2))
-        nc.sync.dma_start(vec_rows[6:8, :], gain.rearrange("(g c) -> g c", g=2))
+        nc.sync.dma_start(vec_rows[4:P:16, :], b1.rearrange("(g q c) -> q g c", g=2, q=4))
+        nc.sync.dma_start(vec_rows[5:P:16, :], gain.rearrange("(g q c) -> q g c", g=2, q=4))
         table = []
 
         def load_table(a):
@@ -116,13 +115,12 @@ def tile_list_telematics_claim_scoring_kernel(
         deal_w1(0, 0, held([P, 2 * PASS], U8, "w1_codes00"))
         deal_w1(0, 1, held([P, 2 * PASS], U8, "w1_codes01"))
 
-        identity = held([P, P], F32, "identity")
-        make_identity(nc, identity[:])
-        turned = psum.tile([P, PACK, P], F32, name="turned", tag="bank7")
-        for t in range(PACK):
-            nc.tensor.transpose(turned[:, t, :], vec_rows[:, t:PASS:PACK], identity[:])
-        vecs = held([P, PACK, 4], F32, "vecs")
-        nc.scalar.copy(vecs[:], turned[:, :, 4:8])
+        vec_dealt = held([P, P], F32, "vec_dealt")
+        nc.vector.tensor_copy(
+            vec_dealt[:].rearrange("p (t i) -> p t i", t=PACK), vec_rows[:].rearrange("p (i t) -> p t i", t=PACK)
+        )
+        vecs = held([P, P], F32, "vecs")
+        nc.vector.transpose(vecs[:], vec_dealt[:])
 
         picked = {}
 
@@ -208,7 +206,7 @@ def tile_list_telematics_claim_scoring_kernel(
                 act[g, half, t] = streamed([P, W], F32, "act11%d" % t, 8 + 2 * t)
             else:
                 act[g, half, t] = held([P, W], F32, "act%d%d%d" % (g, half, t))
-            nc.scalar.activation(act[g, half, t][:], pre[g, half, t][:], ACT.Gelu_apprx_tanh, bias=vecs[:, t, g : g + 1])
+            nc.scalar.activation(act[g, half, t][:], pre[g, half, t][:], ACT.Gelu_apprx_tanh, bias=vecs[:, 32 * t + 16 * g + 4 : 32 * t + 16 * g + 5])
 
         for g in range(2):
             for half in range(2):
@@ -228,7 +226,7 @@ def tile_list_telematics_claim_scoring_kernel(
                     stop=(a == 0),
                 )
             nc.vector.scalar_tensor_tensor(
-                h[g, half][:, t, :], act[g, half, t][:], vecs[:, t, 2 + g : 3 + g], acc[:], ALU.mult, ALU.add
+                h[g, half][:, t, :], act[g, half, t][:], vecs[:, 32 * t + 16 * g + 5 : 32 * t + 16 * g + 6], acc[:], ALU.mult, ALU.add
             )
 
         def store_h(g, half, lo, hi):
@@ -349,8 +347,8 @@ def tile_list_telematics_claim_scoring_kernel(
         stored_pair(1, 0, 2, 6)
         quantize_h(0, 0)
         store_codes(0, 0, W)
-        round_h(1, 0, "scalar", 0, 384)
-        round_h(1, 0, "vector", 384, W)
+        round_h(1, 0, "scalar", 0, 256)
+        round_h(1, 0, "vector", 256, W)
         stored_pair(1, 1, 0, 4)
         stored_pair(1, 1, 2, 0)
         quantize_h(0, 1)

@@ -127,7 +127,10 @@ def tile_list_telematics_claim_scoring_kernel(
         def pick(a):
             for half in range(2):
                 picked[a, half] = held([P, W], U32, "picked%d%d" % (a, half))
-                nc.vector.tensor_copy(picked[a, half][:], table[a][:].bitcast(U32).indirect(half_of_list(half)))
+                step = W // 2 if (a, half) == (1, 0) else W
+                for lo in range(0, W, step):
+                    entries = offsets[:, (half * W + lo) // 16 : (half * W + lo + step) // 16]
+                    nc.vector.tensor_copy(picked[a, half][:, lo : lo + step], table[a][:].bitcast(U32).indirect(entries))
 
         w2_raw = {}
 
@@ -187,18 +190,18 @@ def tile_list_telematics_claim_scoring_kernel(
         h_scales = held([P, 2 * S], U8, "h_scales")
         h_codes = [held([P, S], U32, "h_codes%d" % g) for g in range(2)]
 
-        def w1_pass(g, half, t, a, bank):
+        def w1_pass(g, half, t, a, bank, lo=0, hi=W):
             col = g * PASS + t * P
             if a == 0:
                 pre[g, half, t] = psum.tile([P, W], F32, name="pre%d%d%d" % (g, half, t), tag="bank%d" % bank)
             nc.tensor.matmul_mx(
-                out=pre[g, half, t][:],
+                out=pre[g, half, t][:, lo:hi],
                 lhsT=w1_codes[g, a][:, 2 * t * P : 2 * (t + 1) * P].bitcast(FP4X4),
                 lhsT_scale=planes[:, a * ROW + W10 + col : a * ROW + W10 + col + P],
-                rhs=picked[a, half][:].bitcast(FP8X4),
-                rhs_scale=tab_plane(a, half),
+                rhs=picked[a, half][:, lo:hi].bitcast(FP8X4),
+                rhs_scale=tab_plane(a, half)[:, lo:hi],
                 start=(a == 0),
-                stop=(a == 1),
+                stop=(a == 1 and hi == W),
             )
 
         def gelu(g, half, t):
@@ -302,9 +305,11 @@ def tile_list_telematics_claim_scoring_kernel(
         for g in range(2):
             for t in range(PACK):
                 w1_pass(g, 0, t, 0, PACK * g + t)
+        for t in range(PACK):
+            w1_pass(0, 0, t, 1, t, 0, W // 2)
         for g in range(2):
             for t in range(PACK):
-                w1_pass(g, 0, t, 1, PACK * g + t)
+                w1_pass(g, 0, t, 1, PACK * g + t, W // 2 if g == 0 else 0)
                 gelu(g, 0, t)
         round_w2(0, 0, "vector", "vector")
         load_w2(1, 1)
@@ -350,9 +355,11 @@ def tile_list_telematics_claim_scoring_kernel(
         round_h(1, 0, "scalar", 0, 256)
         round_h(1, 0, "vector", 256, W)
         stored_pair(1, 1, 0, 4)
-        stored_pair(1, 1, 2, 0)
+        feature_tile(1, 1, 2, 0)
         quantize_h(0, 1)
         store_codes(0, W, S)
+        feature_tile(1, 1, 3, 1)
+        store_h(1, 1, 2, PACK)
         quantize_h(1, 0)
         store_codes(1, 0, W)
         round_h(1, 1, "vector", 0, W // 2)

@@ -22,7 +22,6 @@ PASS = P * PACK
 W = 512
 R0 = 96
 TAB0, W10, ROW = 0, W, W + H
-W30, LATE_ROW = W, W + N
 
 
 def tile_list_telematics_claim_scoring_kernel(
@@ -52,8 +51,7 @@ def tile_list_telematics_claim_scoring_kernel(
         w1_rows = held([P, H], U8, "w1_rows")
         rows = held([P, ROW], U8, "rows")
         planes = held([P, 2 * ROW], U8, "planes")
-        late_rows = held([P, LATE_ROW], U8, "late_rows")
-        second_planes = held([P, 2 * LATE_ROW], U8, "second_planes")
+        second_planes = held([P, 2 * W], U8, "second_planes")
         nc.sync.dma_start(w1_rows[R0:P, :].bitcast(I32), scale_rows(w1_scales))
         nc.sync.dma_start(tab_rows[R0:P, :].bitcast(I32), scale_rows(tab_scales))
         w1_raw = held([P, 2 * 2 * H], U8, "w1_raw")
@@ -72,7 +70,6 @@ def tile_list_telematics_claim_scoring_kernel(
             nc.sync.dma_start(table[a][:], tab_words[a].rearrange("p t i -> p (t i)").bitcast(I32), max_dma_last_dim=2048)
 
         load_table(0)
-        nc.sync.dma_start(late_rows[R0:P, W30:LATE_ROW].bitcast(I32), scale_rows(w3_scales))
 
         nc.vector.memset(w1_rows[0:R0, :].bitcast(I32), 0)
         nc.vector.memset(tab_rows[0:R0, :].bitcast(I32), 0)
@@ -146,8 +143,7 @@ def tile_list_telematics_claim_scoring_kernel(
         deal_w1(1, 1, streamed([P, 2 * PASS], U8, "w1_codes11", 2))
         second_rows = streamed([P, W], U8, "second_rows", 3)
         nc.vector.tensor_copy(second_rows[:], tab_rows[:].indirect(half_of_list(1)))
-        nc.vector.tensor_copy(late_rows[R0:P, 0:W].bitcast(I32), second_rows[R0:P, :].bitcast(I32))
-        move_rows(second_planes, late_rows)
+        move_rows(second_planes, second_rows)
         deal_w1(1, 0, streamed([P, 2 * PASS], U8, "w1_codes10", 4))
         pick(1)
 
@@ -184,7 +180,7 @@ def tile_list_telematics_claim_scoring_kernel(
         def tab_plane(a, half):
             if half == 0:
                 return planes[:, a * ROW + TAB0 : a * ROW + W10]
-            return second_planes[:, a * LATE_ROW : a * LATE_ROW + W]
+            return second_planes[:, a * W : (a + 1) * W]
 
         act, h, h_bf, pre = {}, {}, {}, {}
         h_scales = held([P, 2 * S], U8, "h_scales")
@@ -274,7 +270,7 @@ def tile_list_telematics_claim_scoring_kernel(
             nc.tensor.matmul_mx(
                 out=logit[first, i][:],
                 lhsT=w3_codes[:, g * N + i * P : g * N + (i + 1) * P].bitcast(FP8X4),
-                lhsT_scale=second_planes[:, g * LATE_ROW + W30 + i * P : g * LATE_ROW + W30 + (i + 1) * P],
+                lhsT_scale=w3_planes[:, g * N + i * P : g * N + (i + 1) * P],
                 rhs=h_codes[g][:, first : first + width].bitcast(FP8X4),
                 rhs_scale=h_scales[:, g * S + first : g * S + first + width],
                 start=(g == 0),
@@ -325,6 +321,13 @@ def tile_list_telematics_claim_scoring_kernel(
         quantize_w2(0, 1, 1)
         expo = streamed([P, 2, S], F32, "expo", 62)
         nc.sync.dma_start(expo[:], exposure.rearrange("(i p) j -> p i j", p=P))
+        w3_planes = streamed([P, 2 * N], U8, "w3_planes", 37)
+        nc.vector.memset(w3_planes[:].bitcast(I32), 0)
+        for r in range(4):
+            nc.sync.dma_start(
+                w3_planes[r:P:32, :].bitcast(I32).rearrange("p (a c) -> p a c", a=2),
+                w3_scales[:, r:16:4, :].rearrange("a q n -> q a n").bitcast(I32),
+            )
         w1_pair(0, 1, 0, 0)
         w1_pair(0, 1, 2, 2)
         for t in range(PACK):
@@ -350,11 +353,13 @@ def tile_list_telematics_claim_scoring_kernel(
         round_h(0, 1, "scalar")
         stored_pair(1, 0, 0, 2)
         stored_pair(1, 0, 2, 6)
+        round_h(1, 0, "scalar", 0, 384)
+        feature_tile(1, 1, 0, 4)
+        round_h(1, 0, "vector", 384, W)
+        feature_tile(1, 1, 1, 5)
+        store_h(1, 1, 0, 2)
         quantize_h(0, 0)
         store_codes(0, 0, W)
-        round_h(1, 0, "scalar", 0, 256)
-        round_h(1, 0, "vector", 256, W)
-        stored_pair(1, 1, 0, 4)
         feature_tile(1, 1, 2, 0)
         quantize_h(0, 1)
         store_codes(0, W, S)

@@ -148,7 +148,13 @@ def tile_list_telematics_claim_scoring_kernel(
         pick(1)
 
         load_w2(0, 1)
-        load_w2(1, 0)
+        w2_halves = []
+        for n in range(2):
+            w2_halves.append(streamed([P, PACK, PASS // 2], F32, "w2_half%d" % n, 29 - 4 * n))
+            nc.sync.dma_start(
+                w2_halves[n][:],
+                w2[0:PASS, PASS + n * PASS // 2 : PASS + (n + 1) * PASS // 2].rearrange("(p j) c -> p j c", j=PACK),
+            )
 
         w2_bf, w2_codes, w2_scales = {}, {}, {}
 
@@ -164,6 +170,12 @@ def tile_list_telematics_claim_scoring_kernel(
             else:
                 w2_bf[g, a] = streamed([P, PASS * PACK], BF16, "w2_bf%d%d" % (g, a), (33, 37, 72)[2 * g + a])
             dst = w2_bf[g, a][:].rearrange("p (t m j) -> p m j t", t=PACK, j=PACK)
+            if (g, a) == (1, 0):
+                first_half, second_half = (x[:].rearrange("p j (m t) -> p m j t", t=PACK) for x in w2_halves)
+                rounded(first, dst[:, 0 : P // 2], first_half)
+                for lo in (0, 2):
+                    rounded(first, dst[:, P // 2 : P, :, lo : lo + 2], second_half[:, :, :, lo : lo + 2])
+                return
             src = w2_raw[g, a][:].rearrange("p j (m t) -> p m j t", t=PACK)
             for lo, engine in ((0, first), (2, second)):
                 rounded(engine, dst[:, :, :, lo : lo + 2], src[:, :, :, lo : lo + 2])

from contextlib import ExitStack

import concourse.mybir as mybir

K, T, S, H, N = 1024, 4096, 1024, 1024, 256
FLOPS = 2 * (2 * K * H * S + H * N * S)

F32 = mybir.dt.float32
BF16 = mybir.dt.bfloat16
I32 = mybir.dt.int32
U32 = mybir.dt.uint32
U16 = mybir.dt.uint16
U8 = mybir.dt.uint8
FP8X4 = mybir.dt.float8_e4m3fn_x4
FP4X4 = mybir.dt.float4_e2m1fn_x4
ACT = mybir.ActivationFunctionType
ALU = mybir.AluOpType

P = 128
PACK = 4
PASS = P * PACK
W = 512
R0 = 96
TAB0, W10, ROW = 0, W, W + H


def tile_list_telematics_claim_scoring_kernel(
    tc, tab_words, tab_scales, offs, w1_words, w1_scales, b1, gain, w2, w3_words, w3_scales, exposure,
    out_0, out_1, out_2, out_3,
):
    nc = tc.nc
    with ExitStack() as ctx:
        lists = ctx.enter_context(tc.tile_pool(name="lists", bufs=1))
        stream = ctx.enter_context(tc.tile_pool(name="stream", bufs=1))
        keep = ctx.enter_context(tc.tile_pool(name="keep", bufs=1))
        psum = ctx.enter_context(tc.psum_pool(name="psum", bufs=1))

        def held(shape, dtype, name, tag=None):
            return keep.tile(shape, dtype, name=name, tag=tag or name, align_bytes=64)

        def streamed(shape, dtype, name, kib):
            return stream.tile(shape, dtype, name=name, offset=int(kib * 1024), align_bytes=64)

        offsets = lists.tile([P, S // 16], U16, name="offsets")
        nc.sync.dma_start(offsets[:], offs)

        def scale_rows(scales):
            return scales.rearrange("a q n -> q a n").bitcast(I32)

        tab_rows = streamed([P, T], U8, "tab_rows", 60)
        w1_rows = held([P, H], U8, "w1_rows")
        rows = held([P, ROW], U8, "rows")
        planes = held([P, 2 * ROW], U8, "planes")
        second_planes = held([P, 2 * W], U8, "second_planes")
        nc.sync.dma_start(w1_rows[R0:P, :].bitcast(I32), scale_rows(w1_scales))
        nc.sync.dma_start(tab_rows[R0:P, :].bitcast(I32), scale_rows(tab_scales))
        w1_raw = held([P, 2 * 2 * H], U8, "w1_raw")
        nc.sync.dma_start(
            w1_raw[:].bitcast(I32).rearrange("p (a c) -> p a c", a=2),
            w1_words.rearrange("a p c -> p a c").bitcast(I32),
        )
        vec_rows = held([P, P], F32, "vec_rows")
        nc.vector.memset(vec_rows[:].bitcast(I32), 0)
        nc.sync.dma_start(vec_rows[4:P:16, :], b1.rearrange("(g q c) -> q g c", g=2, q=4))
        nc.sync.dma_start(vec_rows[5:P:16, :], gain.rearrange("(g q c) -> q g c", g=2, q=4))
        table = []

        def load_table(a):
            table.append(streamed([P, T], I32, "table%d" % a, 1 + 24 * a))
            nc.sync.dma_start(table[a][:], tab_words[a].rearrange("p t i -> p (t i)").bitcast(I32), max_dma_last_dim=2048)

        load_table(0)

        nc.vector.memset(w1_rows[0:R0, :].bitcast(I32), 0)
        nc.vector.memset(tab_rows[0:R0, :].bitcast(I32), 0)
        nc.vector.memset(planes[:].bitcast(I32), 0)
        nc.vector.memset(second_planes[:].bitcast(I32), 0)


        nc.vector.tensor_copy(
            rows[:, W10:ROW].rearrange("p (g t m) -> p g t m", g=2, t=PACK),
            w1_rows[:].rearrange("p (g m t) -> p g t m", g=2, t=PACK),
        )

        def half_of_list(half):
            return offsets[:, half * W // 16 : (half + 1) * W // 16]

        def move_rows(dst, src):
            for q in (0, 2, 1, 3):
                queue = nc.sync if q < 2 else nc.scalar
                queue.dma_start(
                    dst[32 * q : 32 * q + 4, :].bitcast(I32).rearrange("p (a c) -> p a c", a=2),
                    src[R0 + 8 * q : R0 + 8 * q + 8, :].bitcast(I32),
                )

        first_rows = streamed([P, W], U8, "first_rows", 24.75)
        nc.vector.tensor_copy(first_rows[:], tab_rows[:].indirect(half_of_list(0)))
        nc.vector.tensor_copy(rows[:, TAB0:W10].bitcast(I32), first_rows[:].bitcast(I32))
        move_rows(planes, rows)
        load_table(1)

        w1_codes = {}

        def deal_w1(g, a, codes):
            w1_codes[g, a] = codes
            words = w1_raw[:, 2 * (a * H + g * PASS) : 2 * (a * H + (g + 1) * PASS)]
            nc.vector.tensor_copy(
                codes[:].bitcast(U16).rearrange("p (t m) -> p t m", t=PACK),
                words.bitcast(U16).rearrange("p (m t) -> p t m", t=PACK),
            )

        deal_w1(0, 0, held([P, 2 * PASS], U8, "w1_codes00"))
        deal_w1(0, 1, held([P, 2 * PASS], U8, "w1_codes01"))

        vec_dealt = held([P, P], F32, "vec_dealt")
        nc.vector.tensor_copy(
            vec_dealt[:].rearrange("p (t i) -> p t i", t=PACK), vec_rows[:].rearrange("p (i t) -> p t i", t=PACK)
        )
        vecs = held([P, P], F32, "vecs")
        nc.vector.transpose(vecs[:], vec_dealt[:])

        picked = {}

        def pick(a):
            for half in range(2):
                picked[a, half] = held([P, W], U32, "picked%d%d" % (a, half))
                step = W // 2 if (a, half) == (1, 0) else W
                for lo in range(0, W, step):
                    entries = offsets[:, (half * W + lo) // 16 : (half * W + lo + step) // 16]
                    nc.vector.tensor_copy(picked[a, half][:, lo : lo + step], table[a][:].bitcast(U32).indirect(entries))

        w2_raw = {}

        def load_w2(g, a):
            w2_raw[g, a] = streamed([P, PACK, PASS], F32, "w2_raw%d%d" % (g, a), ((8, 62), (25, 8))[g][a])
            nc.sync.dma_start(
                w2_raw[g, a][:],
                w2[a * PASS : (a + 1) * PASS, g * PASS : (g + 1) * PASS].rearrange("(p j) c -> p j c", j=PACK),
            )

        pick(0)
        load_w2(0, 0)
        deal_w1(1, 1, streamed([P, 2 * PASS], U8, "w1_codes11", 2))
        second_rows = streamed([P, W], U8, "second_rows", 3)
        nc.vector.tensor_copy(second_rows[:], tab_rows[:].indirect(half_of_list(1)))
        move_rows(second_planes, second_rows)
        deal_w1(1, 0, streamed([P, 2 * PASS], U8, "w1_codes10", 4))
        pick(1)

        load_w2(0, 1)
        w2_halves = []
        for n in range(2):
            w2_halves.append(streamed([P, PACK, PASS // 2], F32, "w2_half%d" % n, 29 - 4 * n))
            nc.sync.dma_start(
                w2_halves[n][:],
                w2[0:PASS, PASS + n * PASS // 2 : PASS + (n + 1) * PASS // 2].rearrange("(p j) c -> p j c", j=PACK),
            )

        w2_bf, w2_codes, w2_scales = {}, {}, {}

        def rounded(engine, dst, src):
            if engine == "vector":
                nc.vector.tensor_copy(dst, src)
            else:
                nc.scalar.copy(dst, src)

        def round_w2(g, a, first, second):
            if (g, a) == (1, 1):
                w2_bf[g, a] = held([P, PASS * PACK], BF16, "w2_bf11")
            else:
                w2_bf[g, a] = streamed([P, PASS * PACK], BF16, "w2_bf%d%d" % (g, a), (33, 37, 72)[2 * g + a])
            dst = w2_bf[g, a][:].rearrange("p (t m j) -> p m j t", t=PACK, j=PACK)
            if (g, a) == (1, 0):
                first_half, second_half = (x[:].rearrange("p j (m t) -> p m j t", t=PACK) for x in w2_halves)
                rounded(first, dst[:, 0 : P // 2], first_half)
                for lo in (0, 2):
                    rounded(first, dst[:, P // 2 : P, :, lo : lo + 2], second_half[:, :, :, lo : lo + 2])
                return
            src = w2_raw[g, a][:].rearrange("p j (m t) -> p m j t", t=PACK)
            for lo, engine in ((0, first), (2, second)):
                rounded(engine, dst[:, :, :, lo : lo + 2], src[:, :, :, lo : lo + 2])

        def quantize_w2(g, a, pair, tag=None):
            w2_codes[g, a, pair] = held([P, PASS // 2], U32, "w2_codes%d%d%d" % (g, a, pair), tag)
            w2_scales[g, a, pair] = held([P, PASS // 2], U8, "w2_scales%d%d%d" % (g, a, pair))
            nc.vector.quantize_mx(
                out=w2_codes[g, a, pair][:].bitcast(FP8X4),
                scales=w2_scales[g, a, pair][:],
                in_=w2_bf[g, a][:, pair * 2 * PASS : (pair + 1) * 2 * PASS],
            )

        def tab_plane(a, half):
            if half == 0:
                return planes[:, a * ROW + TAB0 : a * ROW + W10]
            return second_planes[:, a * W : (a + 1) * W]

        act, h, h_bf, pre = {}, {}, {}, {}
        h_scales = held([P, 2 * S], U8, "h_scales")
        h_codes = [held([P, S], U32, "h_codes%d" % g) for g in range(2)]

        def w1_pass(g, half, t, a, bank, lo=0, hi=W):
            col = g * PASS + t * P
            if a == 0:
                pre[g, half, t] = psum.tile([P, W], F32, name="pre%d%d%d" % (g, half, t), tag="bank%d" % bank)
            nc.tensor.matmul_mx(
                out=pre[g, half, t][:, lo:hi],
                lhsT=w1_codes[g, a][:, 2 * t * P : 2 * (t + 1) * P].bitcast(FP4X4),
                lhsT_scale=planes[:, a * ROW + W10 + col : a * ROW + W10 + col + P],
                rhs=picked[a, half][:, lo:hi].bitcast(FP8X4),
                rhs_scale=tab_plane(a, half)[:, lo:hi],
                start=(a == 0),
                stop=(a == 1 and hi == W),
            )

        def gelu(g, half, t):
            if (g, half) == (1, 1) and t >= 2:
                act[g, half, t] = streamed([P, W], F32, "act11%d" % t, 8 + 2 * t)
            else:
                act[g, half, t] = held([P, W], F32, "act%d%d%d" % (g, half, t))
            nc.scalar.activation(act[g, half, t][:], pre[g, half, t][:], ACT.Gelu_apprx_tanh, bias=vecs[:, 32 * t + 16 * g + 4 : 32 * t + 16 * g + 5])

        for g in range(2):
            for half in range(2):
                if (g, half) != (0, 0):
                    h[g, half] = held([P, PACK, W], F32, "h%d%d" % (g, half))

        def feature_tile(g, half, t, bank):
            acc = psum.tile([P, W], F32, name="lin%d%d%d" % (g, half, t), tag="bank%d" % bank)
            for a in (1, 0):
                nc.tensor.matmul_mx(
                    out=acc[:],
                    lhsT=w2_codes[g, a, t // 2][:, t % 2 * P : (t % 2 + 1) * P].bitcast(FP8X4),
                    lhsT_scale=w2_scales[g, a, t // 2][:, t % 2 * P : (t % 2 + 1) * P],
                    rhs=picked[a, half][:].bitcast(FP8X4),
                    rhs_scale=tab_plane(a, half),
                    start=(a == 1),
                    stop=(a == 0),
                )
            nc.vector.scalar_tensor_tensor(
                h[g, half][:, t, :], act[g, half, t][:], vecs[:, 32 * t + 16 * g + 5 : 32 * t + 16 * g + 6], acc[:], ALU.mult, ALU.add
            )

        def store_h(g, half, lo, hi):
            rows_of_group = out_1[g * PASS : (g + 1) * PASS, :].rearrange("(p t) j -> p t j", t=PACK)
            nc.sync.dma_start(rows_of_group[:, lo:hi, half * W : (half + 1) * W], h[g, half][:, lo:hi, :])

        def feature_pair(g, half, lo, bank):
            feature_tile(g, half, lo, bank)
            feature_tile(g, half, lo + 1, bank + 1)

        def stored_pair(g, half, lo, bank):
            feature_pair(g, half, lo, bank)
            store_h(g, half, lo, lo + 2)

        def round_h(g, half, engine, lo=0, hi=W):
            if (g, half) not in h_bf:
                h_bf[g, half] = held([P, W * PACK], BF16, "h_bf%d%d" % (g, half))
            dst = h_bf[g, half][:, lo * PACK : hi * PACK].rearrange("p (c i t) -> p c t i", i=4, t=PACK)
            src = h[g, half][:, :, lo:hi].rearrange("p t (c i) -> p c t i", i=4)
            rounded(engine, dst, src)

        def h_plane(g, half):
            return h_scales[:, g * S + half * W : g * S + (half + 1) * W]

        def quantize_h(g, half, lo=0, hi=W):
            nc.vector.quantize_mx(
                out=h_codes[g][:, half * W + lo : half * W + hi].bitcast(FP8X4),
                scales=h_plane(g, half)[:, lo:hi],
                in_=h_bf[g, half][:, lo * PACK : hi * PACK],
            )

        def store_codes(g, lo, hi):
            nc.sync.dma_start(
                out_2[g].rearrange("p m t -> p (m t)").bitcast(I32)[:, lo:hi], h_codes[g][:, lo:hi].bitcast(I32)
            )

        logit = {}

        def head_pass(first, width, i, g, bank):
            if g == 0:
                logit[first, i] = psum.tile([P, width], F32, name="logit%d_%d" % (first, i), tag="bank%d" % bank)
            nc.tensor.matmul_mx(
                out=logit[first, i][:],
                lhsT=w3_codes[:, g * N + i * P : g * N + (i + 1) * P].bitcast(FP8X4),
                lhsT_scale=w3_planes[:, g * N + i * P : g * N + (i + 1) * P],
                rhs=h_codes[g][:, first : first + width].bitcast(FP8X4),
                rhs_scale=h_scales[:, g * S + first : g * S + first + width],
                start=(g == 0),
                stop=(g == 1),
            )

        def claims_of(first, width, i, claims):
            rate = held([P, width], F32, "rate%d_%d" % (first, i))
            nc.scalar.activation(rate[:], logit[first, i][:], ACT.Exp)
            nc.vector.tensor_tensor(claims[:, i, :], rate[:], expo[:, i, first : first + width], ALU.mult)

        def store_claims(first, width, lo, hi, claims):
            dst = out_0.rearrange("(i p) j -> p i j", p=P)[:, lo:hi, first : first + width]
            nc.sync.dma_start(dst, claims[:, lo:hi, :])

        def store_scales():
            for r in range(4):
                nc.sync.dma_start(
                    out_3[:, r:16:4, :].rearrange("g q j -> q g j").bitcast(I32),
                    h_scales[r:P:32, :].bitcast(I32).rearrange("p (g j) -> p g j", g=2),
                )

        def w1_pair(g, half, lo, bank):
            for t in (lo, lo + 1):
                w1_pass(g, half, t, 0, bank + t - lo)
                w1_pass(g, half, t, 1, bank + t - lo)

        for g in range(2):
            for t in range(PACK):
                w1_pass(g, 0, t, 0, PACK * g + t)
        for t in range(PACK):
            w1_pass(0, 0, t, 1, t, 0, W // 2)
        for g in range(2):
            for t in range(PACK):
                w1_pass(g, 0, t, 1, PACK * g + t, W // 2 if g == 0 else 0)
                gelu(g, 0, t)
        round_w2(0, 0, "vector", "vector")
        load_w2(1, 1)
        quantize_w2(0, 0, 0)
        quantize_w2(0, 0, 1)
        w3_codes = streamed([P, 2 * N], I32, "w3_codes", 33)
        nc.sync.dma_start(
            w3_codes[:].rearrange("p (a c) -> p a c", a=2),
            w3_words.rearrange("a p c i -> p a (c i)").bitcast(I32),
        )
        round_w2(0, 1, "vector", "vector")
        quantize_w2(0, 1, 0)
        quantize_w2(0, 1, 1)
        expo = streamed([P, 2, S], F32, "expo", 62)
        nc.sync.dma_start(expo[:], exposure.rearrange("(i p) j -> p i j", p=P))
        w3_planes = streamed([P, 2 * N], U8, "w3_planes", 37)
        nc.vector.memset(w3_planes[:].bitcast(I32), 0)
        for r in range(4):
            nc.sync.dma_start(
                w3_planes[r:P:32, :].bitcast(I32).rearrange("p (a c) -> p a c", a=2),
                w3_scales[:, r:16:4, :].rearrange("a q n -> q a n").bitcast(I32),
            )
        w1_pair(0, 1, 0, 0)
        w1_pair(0, 1, 2, 2)
        for t in range(PACK):
            gelu(0, 1, t)
        w1_pair(1, 1, 0, 4)
        gelu(1, 1, 0)
        gelu(1, 1, 1)
        round_w2(1, 0, "vector", "vector")
        round_w2(1, 1, "scalar", "scalar")
        h[0, 0] = streamed([P, PACK, W], F32, "h00", 25)
        quantize_w2(1, 0, 0)
        stored_pair(0, 0, 0, 6)
        quantize_w2(1, 0, 1)
        stored_pair(0, 0, 2, 0)
        stored_pair(0, 1, 0, 2)
        quantize_w2(1, 1, 0, "act010")
        stored_pair(0, 1, 2, 6)
        quantize_w2(1, 1, 1, "act012")
        w1_pair(1, 1, 2, 0)
        gelu(1, 1, 2)
        gelu(1, 1, 3)
        round_h(0, 0, "scalar")
        round_h(0, 1, "scalar")
        stored_pair(1, 0, 0, 2)
        stored_pair(1, 0, 2, 6)
        round_h(1, 0, "scalar", 0, 384)
        feature_tile(1, 1, 0, 4)
        round_h(1, 0, "vector", 384, W)
        feature_tile(1, 1, 1, 5)
        store_h(1, 1, 0, 2)
        quantize_h(0, 0)
        store_codes(0, 0, W)
        feature_tile(1, 1, 2, 0)
        quantize_h(0, 1)
        store_codes(0, W, S)
        feature_tile(1, 1, 3, 1)
        store_h(1, 1, 2, PACK)
        quantize_h(1, 0)
        store_codes(1, 0, W)
        round_h(1, 1, "vector", 0, W // 2)
        round_h(1, 1, "vector", W // 2, W)
        quantize_h(1, 1, 0, W // 2)
        store_codes(1, W, W + W // 2)
        quantize_h(1, 1, W // 2, W)
        store_scales()
        store_codes(1, W + W // 2, S)
        spans = ((0, W, 2), (W, W // 2, 6), (W + W // 2, W // 2, 4))
        for first, width, bank in spans:
            for i in range(N // P):
                head_pass(first, width, i, 0, bank + i)
        for first, width, bank in spans:
            claims = held([P, N // P, width], F32, "claims%d" % first)
            for i in range(N // P):
                head_pass(first, width, i, 1, bank + i)
                claims_of(first, width, i, claims)
                if width == W:
                    store_claims(first, width, i, i + 1, claims)
            if width < W:
                store_claims(first, width, 0, N // P, claims)
